import numpy as np
import ml_dtypes


def mxq(x, axis, fmt="e4m3"):
    dtype, down = {"e4m3": (ml_dtypes.float8_e4m3fn, 7), "e5m2": (ml_dtypes.float8_e5m2, 14)}[fmt]
    v = np.moveaxis(np.asarray(x, np.float32).astype(ml_dtypes.bfloat16).astype(np.float64), axis, -1)
    blocks = v.reshape(v.shape[:-1] + (-1, 32))
    amax = np.abs(blocks).max(-1, keepdims=True)
    byte = np.maximum(np.where(amax > 0, np.frexp(amax)[1] - 1 + 127, 0) - down, 1)
    scale = np.exp2(byte - 127.0)
    codes = (blocks / scale).astype(np.float32).astype(dtype).astype(np.float64)
    return np.moveaxis((codes * scale).reshape(v.shape), -1, axis)


WIDE = False


def mx_kscale(k):
    if not WIDE:
        return np.ones(k)
    levels = np.array([10, -10, 5, -5, 0])
    if k % 512:
        return np.exp2(np.random.permutation(np.resize(levels, k // 32))).repeat(32)
    a = np.empty((k // 512, 16))
    for p in range(k // 512):
        a[p, :8] = np.random.permutation(np.resize(levels, 8))
        for g in range(8):
            far = levels[np.abs(levels - a[p, g]) >= 10]
            a[p, g + 8] = far[np.random.randint(len(far))]
    return np.exp2(a.ravel()).repeat(32)


def f64(x):
    return np.asarray(x).astype(np.float64)


def striped(idx):
    return np.tile(idx.reshape(-1, 16).T, (8, 1)).astype(np.uint16)


def unstriped(offs):
    return offs[:16].T.reshape(-1).astype(np.int64)


def pack_weight(w):
    k, n = w.shape
    w = f64(np.asarray(w, np.float32).astype(ml_dtypes.bfloat16)).reshape(k // 32, 32, n)
    amax = np.abs(w).max(1)
    byte = np.clip(np.where(amax > 0, np.frexp(amax)[1] - 1 + 127 - 7, 1), 1, 254)
    scaled = (w * np.exp2(127.0 - byte)[:, None, :]).reshape(k, n).astype(np.float32)
    words = np.ascontiguousarray(scaled.reshape(k // 512, 128, 4, n).transpose(0, 1, 3, 2)).astype(ml_dtypes.float8_e4m3fn).view(np.uint8)
    return words, np.ascontiguousarray(byte.astype(np.uint8).reshape(k // 512, 16, n))


def unpack_weight(words, scales):
    g, p, n, _ = words.shape
    vals = np.ascontiguousarray(words).view(ml_dtypes.float8_e4m3fn).astype(np.float64) * np.repeat(np.exp2(scales.astype(np.float64) - 127.0), 8, axis=1)[..., None]
    return vals.transpose(0, 1, 3, 2).reshape(g * 512, n)


def sigmoid(v):
    return 1.0 / (1.0 + np.exp(-np.maximum(v, -700.0)))


K, T, S, H, N = 512, 2048, 512, 512, 128


def setup_inputs():
    n = np.random.standard_normal
    s = mx_kscale(K)[:, None]
    u = mx_kscale(H)
    packed_xT = pack_weight(n((K, T)) * s)
    packed_gT = pack_weight(n((K, T)) * s)
    packed_dT = pack_weight(n((K, T)) * s)
    packed_eT = pack_weight(n((K, T)) * s)
    return {
        "x_words": packed_xT[0],
        "x_scales": packed_xT[1],
        "g_words": packed_gT[0],
        "g_scales": packed_gT[1],
        "d_words": packed_dT[0],
        "d_scales": packed_dT[1],
        "e_words": packed_eT[0],
        "e_scales": packed_eT[1],
        "w1": (n((K, H)) / np.sqrt(K) / s).astype(np.float32),
        "w2": (n((K, N)) / np.sqrt(K) / s).astype(np.float32),
        "w3": (n((K, N)) / np.sqrt(K) / s).astype(np.float32),
        "w4": (n((H, N)) / np.sqrt(2 * H) / u[:, None]).astype(np.float32),
        "w5": (n((K, N)) / np.sqrt(2 * K) / s).astype(np.float32),
        "gain": (np.random.uniform(0.5, 1.0, (H, 1)) * u[:, None]).astype(np.float32),
        "skip": (n((N, S))).astype(np.float32),
        "offs": striped(np.random.permutation(T)[:S]),
    }


def reference(x_words, x_scales, g_words, g_scales, d_words, d_scales, e_words, e_scales, w1, w2, w3, w4, w5, gain, skip, offs):
    xq = unpack_weight(x_words, x_scales)[:, unstriped(offs)]
    w1q = mxq(f64(w1), 0, "e4m3")
    vx = w1q.T @ xq
    g_offs = unpack_weight(g_words, g_scales)[:, unstriped(offs)]
    vy = w1q.T @ g_offs
    d_offs = unpack_weight(d_words, d_scales)[:, unstriped(offs)]
    vz = w1q.T @ d_offs
    nrm = f64(gain) * (np.sqrt((vx) ** 2 + (vy) ** 2 + (vz) ** 2 + 0.05))
    e_offs = unpack_weight(e_words, e_scales)[:, unstriped(offs)]
    gate = mxq(f64(w4), 0, "e4m3").T @ mxq(nrm, 0, "e4m3") + mxq(f64(w5), 0, "e4m3").T @ e_offs
    w2q = mxq(f64(w2), 0, "e4m3")
    ax = w2q.T @ xq
    w3q = mxq(f64(w3), 0, "e4m3")
    bx = w3q.T @ xq
    ay = w2q.T @ g_offs
    by = w3q.T @ g_offs
    az = w2q.T @ d_offs
    bz = w3q.T @ d_offs
    dot = ax * bx + ay * by + az * bz
    return sigmoid(gate) * (0.5 * dot) + f64(skip)

@@ -1,0 +1,205 @@
+from contextlib import ExitStack
+
+import concourse.mybir as mybir
+from concourse.masks import make_identity
+
+F32 = mybir.dt.float32
+BF16 = mybir.dt.bfloat16
+I32 = mybir.dt.int32
+U32 = mybir.dt.uint32
+U16 = mybir.dt.uint16
+U8 = mybir.dt.uint8
+FP8X4 = mybir.dt.float8_e4m3fn_x4
+ACT = mybir.ActivationFunctionType
+ALU = mybir.AluOpType
+
+P = 128
+PACK = 4
+K, T, S, H, N = 512, 2048, 512, 512, 128
+HALF = S // 2
+TILES = S // P
+FLOPS = 2 * K * S * (3 * H + 7 * N) + 2 * H * S * N
+
+
+def tile_picked_ypainn_sigmoid_p_kernel(
+    tc, x_words, x_scales, g_words, g_scales, d_words, d_scales, e_words, e_scales,
+    w1, w2, w3, w4, w5, gain, skip, offs, out,
+):
+    nc = tc.nc
+    words_in = (x_words, g_words, d_words, e_words)
+    scales_in = (x_scales, g_scales, d_scales, e_scales)
+
+    with ExitStack() as ctx:
+        keep = ctx.enter_context(tc.tile_pool(name="keep", bufs=1))
+        ring = ctx.enter_context(tc.tile_pool(name="ring", bufs=1))
+        psum = ctx.enter_context(tc.psum_pool(name="psum", bufs=1))
+
+        offsets = keep.tile([P, S // 16], U16, name="offsets")
+        nc.sync.dma_start(offsets[:], offs)
+
+        word_win = [keep.tile([P, T], I32, name="word_win%d" % c, align_bytes=64) for c in range(4)]
+        scale_win = [keep.tile([P, T], U8, name="scale_win%d" % c, align_bytes=64) for c in range(4)]
+        nc.vector.memset(scale_win[0][:].bitcast(I32), 0)
+        nc.gpsimd.memset(scale_win[1][:].bitcast(I32), 0)
+        nc.vector.memset(scale_win[2][:].bitcast(I32), 0)
+        nc.vector.memset(scale_win[3][:].bitcast(I32), 0)
+
+        warm = keep.tile([P, 1], F32, name="warm")
+        nc.vector.memset(warm[:], 1.0)
+        warm_out = keep.tile([P, 1], F32, name="warm_out")
+        nc.scalar.activation(warm_out[:], warm[:], ACT.Sqrt)
+
+        def load_scales(queue, c):
+            for r in range(4):
+                queue.dma_start(
+                    scale_win[c][4 * c + r : P : 32, :].bitcast(I32),
+                    scales_in[c][0, r:16:4, :].bitcast(I32),
+                )
+
+        def load_words(c):
+            nc.sync.dma_start(word_win[c][:], words_in[c][0].rearrange("p n t -> p (n t)").bitcast(I32))
+
+        def load_weight(w, cols, name):
+            width = cols.stop - cols.start
+            raw = keep.tile([P, PACK, width], F32, name=name)
+            nc.sync.dma_start(raw[:], w.rearrange("(p j) c -> p j c", j=PACK)[:, :, cols])
+            return raw
+
+        w1_raw = [load_weight(w1, slice(h * 256, (h + 1) * 256), "w1_raw%d" % h) for h in range(2)]
+        load_scales(nc.sync, 0)
+        load_scales(nc.gpsimd, 1)
+        ident = keep.tile([P, P], F32, name="ident")
+        make_identity(nc, ident[:])
+        load_words(0)
+        w2_raw = load_weight(w2, slice(0, N), "w2_raw")
+        w3_raw = load_weight(w3, slice(0, N), "w3_raw")
+        load_words(1)
+        load_scales(nc.sync, 2)
+        load_words(2)
+        gain_t = keep.tile([P, PACK], F32, name="gain_t")
+        nc.sync.dma_start(gain_t[:], gain.rearrange("(p j) o -> p (j o)", j=PACK))
+        load_scales(nc.sync, 3)
+        load_words(3)
+        w4_raw = load_weight(w4, slice(0, N), "w4_raw")
+        w5_raw = load_weight(w5, slice(0, N), "w5_raw")
+        skip_t = keep.tile([P, S], F32, name="skip_t")
+        nc.sync.dma_start(skip_t[:], skip)
+
+        def views(grouped, raw):
+            return (grouped.rearrange("p (c i t) -> p c t i", i=4, t=PACK),
+                    raw.rearrange("p t (c i) -> p c t i", i=4))
+
+        def cast_scalar(grouped, raw):
+            dst, src = views(grouped, raw)
+            nc.scalar.copy(dst, src)
+
+        def cast_vector(grouped, raw):
+            dst, src = views(grouped, raw)
+            nc.vector.tensor_copy(dst, src)
+
+        w1_codes = keep.tile([P, H], U32, name="w1_codes", align_bytes=64)
+        w1_scale = keep.tile([P, H], U8, name="w1_scale", align_bytes=64)
+        for h in range(2):
+            grouped = keep.tile([P, 256 * PACK], BF16, name="w1_bf%d" % h, align_bytes=64)
+            cast_scalar(grouped[:], w1_raw[h][:])
+            cols = slice(h * 256, (h + 1) * 256)
+            nc.vector.quantize_mx(out=w1_codes[:, cols].bitcast(FP8X4), scales=w1_scale[:, cols], in_=grouped[:])
+
+        def quantize_pair(raws, name):
+            grouped = keep.tile([P, 2 * N * PACK], BF16, name=name + "_bf", align_bytes=64)
+            for i, raw in enumerate(raws):
+                cast_vector(grouped[:, i * N * PACK : (i + 1) * N * PACK], raw[:])
+            codes = keep.tile([P, 2 * N], U32, name=name + "_codes", align_bytes=64)
+            scale = keep.tile([P, 2 * N], U8, name=name + "_scale", align_bytes=64)
+            nc.vector.quantize_mx(out=codes[:].bitcast(FP8X4), scales=scale[:], in_=grouped[:])
+            return codes, scale
+
+        def gather_scales(c):
+            picked = keep.tile([P, S], U8, name="picked_scale%d" % c, align_bytes=64)
+            nc.vector.tensor_copy(picked[:], scale_win[c][:].indirect(offsets[:]))
+            return picked
+
+        def gather_words(c, h):
+            picked = keep.tile([P, HALF], U32, name="picked_words%d_%d" % (c, h), align_bytes=64)
+            cols = slice(h * HALF // 16, (h + 1) * HALF // 16)
+            nc.vector.tensor_copy(picked[:], word_win[c][:].bitcast(U32).indirect(offsets[:, cols]))
+            return picked
+
+        picked_scale = [gather_scales(c) for c in range(2)]
+        sums = [psum.tile([P, PACK, P], F32, name="sum%d" % j, tag="sum%d" % j) for j in range(TILES)]
+        nrm_codes = keep.tile([P, S], U32, name="nrm_codes", align_bytes=64)
+        nrm_scale = keep.tile([P, S], U8, name="nrm_scale", align_bytes=64)
+        prods = {}
+        w23 = None
+
+        def finish_tile(j):
+            root = ring.tile([P, P, PACK], F32, name="root", tag="root", bufs=4)
+            nc.scalar.activation(root[:], sums[j][:].rearrange("p t n -> p n t"), ACT.Sqrt, bias=0.05)
+            nrm = ring.tile([P, P, PACK], BF16, name="nrm", tag="nrm", bufs=4, align_bytes=64)
+            nc.vector.tensor_tensor(nrm[:], root[:], gain_t[:].unsqueeze(1).to_broadcast([P, P, PACK]), ALU.mult)
+            cols = slice(j * P, (j + 1) * P)
+            nc.vector.quantize_mx(out=nrm_codes[:, cols].bitcast(FP8X4), scales=nrm_scale[:, cols],
+                                  in_=nrm[:].rearrange("p n t -> p (n t)"))
+
+        for c in range(3):
+            if c == 2:
+                picked_scale.append(gather_scales(2))
+            picked = [gather_words(c, h) for h in range(2)]
+            if c == 0:
+                w23 = quantize_pair((w2_raw, w3_raw), "w23")
+            for j in range(TILES):
+                h, jj = divmod(j, 2)
+                v = psum.tile([P, H], F32, name="v", tag="v", bufs=2)
+                nc.tensor.matmul_mx(
+                    out=v[:], lhsT=picked[h][:, jj * P : (jj + 1) * P].bitcast(FP8X4),
+                    lhsT_scale=picked_scale[c][4 * c : P, j * P : (j + 1) * P],
+                    rhs=w1_codes[:].bitcast(FP8X4), rhs_scale=w1_scale[:], start=True, stop=True)
+                sq = ring.tile([P, PACK, P], F32, name="sq", tag="sq", bufs=6)
+                nc.scalar.activation(sq[:], v[:].rearrange("p (m t) -> p t m", t=PACK), ACT.Square)
+                for t in range(PACK):
+                    nc.tensor.matmul(out=sums[j][:, t, :], lhsT=sq[:, t, :], rhs=ident[:], is_transpose=True,
+                                     start=(c == 0 and t == 0), stop=(c == 2 and t == PACK - 1))
+            if c == 2:
+                for j in range(TILES):
+                    finish_tile(j)
+            for h in range(2):
+                ab = psum.tile([P, 2, HALF], F32, name="ab", tag="ab", bufs=2)
+                for i in range(2):
+                    nc.tensor.matmul_mx(
+                        out=ab[:, i, :], lhsT=w23[0][:, i * N : (i + 1) * N].bitcast(FP8X4),
+                        lhsT_scale=w23[1][:, i * N : (i + 1) * N],
+                        rhs=picked[h][:].bitcast(FP8X4),
+                        rhs_scale=picked_scale[c][4 * c : P, h * HALF : (h + 1) * HALF], start=True, stop=True)
+                b_half = ring.tile([P, HALF], F32, name="b_half", tag="b_half", bufs=2)
+                nc.scalar.activation(b_half[:], ab[:, 1, :], ACT.Copy, scale=0.5)
+                prod = keep.tile([P, HALF], F32, name="prod%d_%d" % (c, h))
+                nc.vector.tensor_tensor(prod[:], ab[:, 0, :], b_half[:], ALU.mult)
+                prods[c, h] = prod
+                if c == 1:
+                    both = keep.tile([P, HALF], F32, name="both%d" % h)
+                    nc.vector.tensor_tensor(both[:], prods[0, h][:], prod[:], ALU.add)
+                    prods["xy", h] = both
+                if c == 2:
+                    dot = keep.tile([P, HALF], F32, name="dot%d" % h)
+                    nc.vector.tensor_tensor(dot[:], prods["xy", h][:], prod[:], ALU.add)
+                    prods["dot", h] = dot
+
+        e_scale = gather_scales(3)
+        e_picked = [gather_words(3, h) for h in range(2)]
+        w45 = quantize_pair((w4_raw, w5_raw), "w45")
+        for h in range(2):
+            cols = slice(h * HALF, (h + 1) * HALF)
+            gate = psum.tile([P, HALF], F32, name="gate%d" % h, tag="sum%d" % (3 - h))
+            nc.tensor.matmul_mx(out=gate[:], lhsT=w45[0][:, N : 2 * N].bitcast(FP8X4), lhsT_scale=w45[1][:, N : 2 * N],
+                                rhs=e_picked[h][:].bitcast(FP8X4), rhs_scale=e_scale[12:P, cols],
+                                start=True, stop=False)
+            nc.tensor.matmul_mx(out=gate[:], lhsT=w45[0][:, 0:N].bitcast(FP8X4), lhsT_scale=w45[1][:, 0:N],
+                                rhs=nrm_codes[:, cols].bitcast(FP8X4), rhs_scale=nrm_scale[:, cols],
+                                start=False, stop=True)
+            sig = keep.tile([P, HALF], F32, name="sig%d" % h)
+            nc.scalar.activation(sig[:], gate[:], ACT.Sigmoid)
+            gated = keep.tile([P, HALF], F32, name="gated%d" % h)
+            nc.vector.tensor_tensor(gated[:], sig[:], prods["dot", h][:], ALU.mult)
+            res = keep.tile([P, HALF], F32, name="res%d" % h)
+            nc.vector.tensor_tensor(res[:], gated[:], skip_t[:, cols], ALU.add)
+            nc.sync.dma_start(out[:, cols], res[:])

@@ -30,28 +30,31 @@ def tile_picked_ypainn_sigmoid_p_kernel(
     scales_in = (x_scales, g_scales, d_scales, e_scales)
 
     with ExitStack() as ctx:
-        keep = ctx.enter_context(tc.tile_pool(name="keep", bufs=1))
+        first = ctx.enter_context(tc.tile_pool(name="first", bufs=1))
         ring = ctx.enter_context(tc.tile_pool(name="ring", bufs=1))
         psum = ctx.enter_context(tc.psum_pool(name="psum", bufs=1))
 
-        offsets = keep.tile([P, S // 16], U16, name="offsets")
+        offsets = first.tile([P, S // 16], U16, name="offsets")
         nc.sync.dma_start(offsets[:], offs)
 
-        word_win = [keep.tile([P, T], I32, name="word_win%d" % c, align_bytes=64) for c in range(4)]
-        scale_win = [keep.tile([P, T], U8, name="scale_win%d" % c, align_bytes=64) for c in range(4)]
-        nc.vector.memset(scale_win[0][:].bitcast(I32), 0)
-        nc.gpsimd.memset(scale_win[1][:].bitcast(I32), 0)
-        nc.vector.memset(scale_win[2][:].bitcast(I32), 0)
-        nc.vector.memset(scale_win[3][:].bitcast(I32), 0)
+        scale_win = [first.tile([P, T], U8, name="scale_win%d" % c, tag="scale_win%d" % c, align_bytes=64) for c in range(4)]
+        for c in range(4):
+            (nc.vector if c % 2 == 0 else nc.gpsimd).memset(scale_win[c][:].bitcast(I32), 0)
 
-        warm = keep.tile([P, 1], F32, name="warm")
-        nc.vector.memset(warm[:], 1.0)
-        warm_out = keep.tile([P, 1], F32, name="warm_out")
-        nc.scalar.activation(warm_out[:], warm[:], ACT.Sqrt)
+        ident = first.tile([P, P], F32, name="ident")
+        w1_raw = [first.tile([P, PACK, 256], F32, name="w1_raw%d" % h) for h in range(2)]
+        w1_bf = first.tile([P, H * PACK], BF16, name="w1_bf", align_bytes=64)
+        with tc.tile_pool(name="warm", bufs=1) as warm_pool:
+            warm = warm_pool.tile([P, 2], F32, name="warm")
+            nc.gpsimd.memset(warm[:, 0:1], 1.0)
+            nc.scalar.activation(warm[:, 1:2], warm[:, 0:1], ACT.Sqrt)
+        make_identity(nc, ident[:])
+        keep = ctx.enter_context(tc.tile_pool(name="keep", bufs=1))
+        word_win = [keep.tile([P, T], I32, name="word_win%d" % c, tag="win%d" % c, align_bytes=64) for c in range(4)]
 
-        def load_scales(queue, c):
+        def load_scales(c):
             for r in range(4):
-                queue.dma_start(
+                nc.sync.dma_start(
                     scale_win[c][4 * c + r : P : 32, :].bitcast(I32),
                     scales_in[c][0, r:16:4, :].bitcast(I32),
                 )
@@ -65,23 +68,22 @@ def tile_picked_ypainn_sigmoid_p_kernel(
             nc.sync.dma_start(raw[:], w.rearrange("(p j) c -> p j c", j=PACK)[:, :, cols])
             return raw
 
-        w1_raw = [load_weight(w1, slice(h * 256, (h + 1) * 256), "w1_raw%d" % h) for h in range(2)]
-        load_scales(nc.sync, 0)
-        load_scales(nc.gpsimd, 1)
-        ident = keep.tile([P, P], F32, name="ident")
-        make_identity(nc, ident[:])
+        for h in range(2):
+            nc.sync.dma_start(w1_raw[h][:], w1.rearrange("(p j) c -> p j c", j=PACK)[:, :, h * 256 : (h + 1) * 256])
+        load_scales(0)
         load_words(0)
-        w2_raw = load_weight(w2, slice(0, N), "w2_raw")
-        w3_raw = load_weight(w3, slice(0, N), "w3_raw")
-        load_words(1)
-        load_scales(nc.sync, 2)
-        load_words(2)
         gain_t = keep.tile([P, PACK], F32, name="gain_t")
         nc.sync.dma_start(gain_t[:], gain.rearrange("(p j) o -> p (j o)", j=PACK))
-        load_scales(nc.sync, 3)
-        load_words(3)
+        load_scales(1)
+        load_words(1)
+        load_scales(2)
+        load_words(2)
+        w2_raw = load_weight(w2, slice(0, N), "w2_raw")
+        w3_raw = load_weight(w3, slice(0, N), "w3_raw")
+        load_scales(3)
         w4_raw = load_weight(w4, slice(0, N), "w4_raw")
         w5_raw = load_weight(w5, slice(0, N), "w5_raw")
+        load_words(3)
         skip_t = keep.tile([P, S], F32, name="skip_t")
         nc.sync.dma_start(skip_t[:], skip)
 
@@ -89,117 +91,113 @@ def tile_picked_ypainn_sigmoid_p_kernel(
             return (grouped.rearrange("p (c i t) -> p c t i", i=4, t=PACK),
                     raw.rearrange("p t (c i) -> p c t i", i=4))
 
-        def cast_scalar(grouped, raw):
-            dst, src = views(grouped, raw)
-            nc.scalar.copy(dst, src)
-
-        def cast_vector(grouped, raw):
-            dst, src = views(grouped, raw)
-            nc.vector.tensor_copy(dst, src)
-
-        w1_codes = keep.tile([P, H], U32, name="w1_codes", align_bytes=64)
+        w1_codes = first.tile([P, H], U32, name="w1_codes", tag="scale_win0", align_bytes=64)
         w1_scale = keep.tile([P, H], U8, name="w1_scale", align_bytes=64)
         for h in range(2):
-            grouped = keep.tile([P, 256 * PACK], BF16, name="w1_bf%d" % h, align_bytes=64)
-            cast_scalar(grouped[:], w1_raw[h][:])
-            cols = slice(h * 256, (h + 1) * 256)
-            nc.vector.quantize_mx(out=w1_codes[:, cols].bitcast(FP8X4), scales=w1_scale[:, cols], in_=grouped[:])
+            dst, src = views(w1_bf[:, h * 256 * PACK : (h + 1) * 256 * PACK], w1_raw[h][:])
+            nc.scalar.copy(dst, src)
+        nc.vector.quantize_mx(out=w1_codes[:].bitcast(FP8X4), scales=w1_scale[:], in_=w1_bf[:])
 
-        def quantize_pair(raws, name):
-            grouped = keep.tile([P, 2 * N * PACK], BF16, name=name + "_bf", align_bytes=64)
+        def quantize_pair(raws, grouped, name):
             for i, raw in enumerate(raws):
-                cast_vector(grouped[:, i * N * PACK : (i + 1) * N * PACK], raw[:])
+                dst, src = views(grouped[:, i * N * PACK : (i + 1) * N * PACK], raw[:])
+                nc.vector.tensor_copy(dst, src)
             codes = keep.tile([P, 2 * N], U32, name=name + "_codes", align_bytes=64)
             scale = keep.tile([P, 2 * N], U8, name=name + "_scale", align_bytes=64)
             nc.vector.quantize_mx(out=codes[:].bitcast(FP8X4), scales=scale[:], in_=grouped[:])
             return codes, scale
 
         def gather_scales(c):
-            picked = keep.tile([P, S], U8, name="picked_scale%d" % c, align_bytes=64)
-            nc.vector.tensor_copy(picked[:], scale_win[c][:].indirect(offsets[:]))
-            return picked
+            scale = keep.tile([P, S], U8, name="picked_scale%d" % c, tag="win%d" % (c - 1), align_bytes=64)
+            nc.vector.tensor_copy(scale[:], scale_win[c][:].indirect(offsets[:]))
+            return scale
 
-        def gather_words(c, h):
-            picked = keep.tile([P, HALF], U32, name="picked_words%d_%d" % (c, h), align_bytes=64)
-            cols = slice(h * HALF // 16, (h + 1) * HALF // 16)
-            nc.vector.tensor_copy(picked[:], word_win[c][:].bitcast(U32).indirect(offsets[:, cols]))
-            return picked
+        def gather_words(c, pieces, words):
+            width = S // pieces
+            for h in range(pieces):
+                cols = slice(h * width // 16, (h + 1) * width // 16)
+                nc.vector.tensor_copy(words[:, h * width : (h + 1) * width],
+                                      word_win[c][:].bitcast(U32).indirect(offsets[:, cols]))
+            return words
 
-        picked_scale = [gather_scales(c) for c in range(2)]
         sums = [psum.tile([P, PACK, P], F32, name="sum%d" % j, tag="sum%d" % j) for j in range(TILES)]
+        picked = []
+        for c in range(3):
+            scale = gather_scales(c)
+            words = gather_words(c, 1 if c == 1 else 2,
+                                 keep.tile([P, S], U32, name="picked_words%d" % c, align_bytes=64))
+            picked.append((words, scale))
+            squares = []
+            for j in range(TILES):
+                tok = slice(j * P, (j + 1) * P)
+                v = psum.tile([P, H], F32, name="v", tag="work", bufs=4)
+                nc.tensor.matmul_mx(
+                    out=v[:], lhsT=words[:, tok].bitcast(FP8X4), lhsT_scale=scale[4 * c : P, tok],
+                    rhs=w1_codes[:].bitcast(FP8X4), rhs_scale=w1_scale[:], start=True, stop=True)
+                sq = ring.tile([P, PACK, P], F32, name="sq", tag="sq", bufs=8)
+                nc.scalar.activation(sq[:], v[:].rearrange("p (m t) -> p t m", t=PACK), ACT.Square)
+                squares.append(sq)
+            for j in range(TILES):
+                for t in range(PACK):
+                    nc.tensor.matmul(out=sums[j][:, t, :], lhsT=squares[j][:, t, :], rhs=ident[:], is_transpose=True,
+                                     start=(c == 0 and t == 0), stop=(c == 2 and t == PACK - 1))
+
+        roots = []
+        for j in range(TILES):
+            root = keep.tile([P, P, PACK], F32, name="root%d" % j, tag="root%d" % j)
+            nc.scalar.activation(root[:], sums[j][:].rearrange("p t n -> p n t"), ACT.Sqrt, bias=0.05)
+            roots.append(root)
+
+        w23 = quantize_pair((w2_raw, w3_raw), keep.tile([P, 2 * N * PACK], BF16, name="w23_bf", tag="win2", align_bytes=64), "w23")
+        e_scale = gather_scales(3)
+        w45 = quantize_pair((w4_raw, w5_raw), first.tile([P, 2 * N * PACK], BF16, name="w45_bf", tag="scale_win3", align_bytes=64), "w45")
+        e_picked = gather_words(3, 1, first.tile([P, S], U32, name="picked_words3", tag="scale_win3", align_bytes=64))
+
+        nrm = keep.tile([P, TILES, P, PACK], BF16, name="nrm", tag="win3", align_bytes=64)
         nrm_codes = keep.tile([P, S], U32, name="nrm_codes", align_bytes=64)
         nrm_scale = keep.tile([P, S], U8, name="nrm_scale", align_bytes=64)
-        prods = {}
-        w23 = None
-
-        def finish_tile(j):
-            root = ring.tile([P, P, PACK], F32, name="root", tag="root", bufs=4)
-            nc.scalar.activation(root[:], sums[j][:].rearrange("p t n -> p n t"), ACT.Sqrt, bias=0.05)
-            nrm = ring.tile([P, P, PACK], BF16, name="nrm", tag="nrm", bufs=4, align_bytes=64)
-            nc.vector.tensor_tensor(nrm[:], root[:], gain_t[:].unsqueeze(1).to_broadcast([P, P, PACK]), ALU.mult)
-            cols = slice(j * P, (j + 1) * P)
-            nc.vector.quantize_mx(out=nrm_codes[:, cols].bitcast(FP8X4), scales=nrm_scale[:, cols],
-                                  in_=nrm[:].rearrange("p n t -> p (n t)"))
-
-        for c in range(3):
-            if c == 2:
-                picked_scale.append(gather_scales(2))
-            picked = [gather_words(c, h) for h in range(2)]
-            if c == 0:
-                w23 = quantize_pair((w2_raw, w3_raw), "w23")
-            for j in range(TILES):
-                h, jj = divmod(j, 2)
-                v = psum.tile([P, H], F32, name="v", tag="v", bufs=2)
-                nc.tensor.matmul_mx(
-                    out=v[:], lhsT=picked[h][:, jj * P : (jj + 1) * P].bitcast(FP8X4),
-                    lhsT_scale=picked_scale[c][4 * c : P, j * P : (j + 1) * P],
-                    rhs=w1_codes[:].bitcast(FP8X4), rhs_scale=w1_scale[:], start=True, stop=True)
-                sq = ring.tile([P, PACK, P], F32, name="sq", tag="sq", bufs=6)
-                nc.scalar.activation(sq[:], v[:].rearrange("p (m t) -> p t m", t=PACK), ACT.Square)
-                for t in range(PACK):
-                    nc.tensor.matmul(out=sums[j][:, t, :], lhsT=sq[:, t, :], rhs=ident[:], is_transpose=True,
-                                     start=(c == 0 and t == 0), stop=(c == 2 and t == PACK - 1))
-            if c == 2:
-                for j in range(TILES):
-                    finish_tile(j)
-            for h in range(2):
-                ab = psum.tile([P, 2, HALF], F32, name="ab", tag="ab", bufs=2)
-                for i in range(2):
-                    nc.tensor.matmul_mx(
-                        out=ab[:, i, :], lhsT=w23[0][:, i * N : (i + 1) * N].bitcast(FP8X4),
-                        lhsT_scale=w23[1][:, i * N : (i + 1) * N],
-                        rhs=picked[h][:].bitcast(FP8X4),
-                        rhs_scale=picked_scale[c][4 * c : P, h * HALF : (h + 1) * HALF], start=True, stop=True)
-                b_half = ring.tile([P, HALF], F32, name="b_half", tag="b_half", bufs=2)
-                nc.scalar.activation(b_half[:], ab[:, 1, :], ACT.Copy, scale=0.5)
-                prod = keep.tile([P, HALF], F32, name="prod%d_%d" % (c, h))
-                nc.vector.tensor_tensor(prod[:], ab[:, 0, :], b_half[:], ALU.mult)
-                prods[c, h] = prod
-                if c == 1:
-                    both = keep.tile([P, HALF], F32, name="both%d" % h)
-                    nc.vector.tensor_tensor(both[:], prods[0, h][:], prod[:], ALU.add)
-                    prods["xy", h] = both
-                if c == 2:
-                    dot = keep.tile([P, HALF], F32, name="dot%d" % h)
-                    nc.vector.tensor_tensor(dot[:], prods["xy", h][:], prod[:], ALU.add)
-                    prods["dot", h] = dot
-
-        e_scale = gather_scales(3)
-        e_picked = [gather_words(3, h) for h in range(2)]
-        w45 = quantize_pair((w4_raw, w5_raw), "w45")
         for h in range(2):
+            for j in (2 * h, 2 * h + 1):
+                nc.vector.tensor_tensor(nrm[:, j], roots[j][:], gain_t[:].unsqueeze(1).to_broadcast([P, P, PACK]), ALU.mult)
             cols = slice(h * HALF, (h + 1) * HALF)
-            gate = psum.tile([P, HALF], F32, name="gate%d" % h, tag="sum%d" % (3 - h))
-            nc.tensor.matmul_mx(out=gate[:], lhsT=w45[0][:, N : 2 * N].bitcast(FP8X4), lhsT_scale=w45[1][:, N : 2 * N],
-                                rhs=e_picked[h][:].bitcast(FP8X4), rhs_scale=e_scale[12:P, cols],
-                                start=True, stop=False)
-            nc.tensor.matmul_mx(out=gate[:], lhsT=w45[0][:, 0:N].bitcast(FP8X4), lhsT_scale=w45[1][:, 0:N],
-                                rhs=nrm_codes[:, cols].bitcast(FP8X4), rhs_scale=nrm_scale[:, cols],
-                                start=False, stop=True)
-            sig = keep.tile([P, HALF], F32, name="sig%d" % h)
-            nc.scalar.activation(sig[:], gate[:], ACT.Sigmoid)
-            gated = keep.tile([P, HALF], F32, name="gated%d" % h)
-            nc.vector.tensor_tensor(gated[:], sig[:], prods["dot", h][:], ALU.mult)
-            res = keep.tile([P, HALF], F32, name="res%d" % h)
-            nc.vector.tensor_tensor(res[:], gated[:], skip_t[:, cols], ALU.add)
-            nc.sync.dma_start(out[:, cols], res[:])
+            nc.vector.quantize_mx(out=nrm_codes[:, cols].bitcast(FP8X4), scales=nrm_scale[:, cols],
+                                  in_=nrm[:, 2 * h : 2 * h + 2].rearrange("p a n t -> p (a n t)"))
+
+        dot = psum.tile([P, S], F32, name="dot", tag="sum0")
+        for c in range(3):
+            words, scale = picked[c]
+            for h in range(2):
+                step = 2 * c + h
+                if step < 4:
+                    ab = psum.tile([P, 2, 2 * N], F32, name="ab", tag="work", bufs=4)
+                else:
+                    ab = psum.tile([P, 2, 2 * N], F32, name="ab", tag="sum%d" % (step - 3))
+                for jj in range(2):
+                    tok = slice((2 * h + jj) * P, (2 * h + jj + 1) * P)
+                    nc.tensor.matmul_mx(
+                        out=ab[:, jj, :], lhsT=words[:, tok].bitcast(FP8X4), lhsT_scale=scale[4 * c : P, tok],
+                        rhs=w23[0][:].bitcast(FP8X4), rhs_scale=w23[1][:], start=True, stop=True)
+                b_half = keep.tile([P, 2, N], F32, name="b_half%d" % step)
+                nc.scalar.activation(b_half[:], ab[:, :, N : 2 * N], ACT.Copy, scale=0.5)
+                prod = keep.tile([P, 2, N], F32, name="prod%d" % step, tag="root%d" % (step % TILES))
+                nc.vector.tensor_tensor(prod[:], ab[:, :, 0:N], b_half[:], ALU.mult)
+                for jj in range(2):
+                    tok = slice((2 * h + jj) * P, (2 * h + jj + 1) * P)
+                    nc.tensor.matmul(out=dot[:, tok], lhsT=prod[:, jj, :], rhs=ident[:], is_transpose=True,
+                                     start=(step == 0 and jj == 0), stop=(step == 5 and jj == 1))
+
+        gate = psum.tile([P, S], F32, name="gate", tag="sum3")
+        nc.tensor.matmul_mx(out=gate[:], lhsT=w45[0][:, N : 2 * N].bitcast(FP8X4), lhsT_scale=w45[1][:, N : 2 * N],
+                            rhs=e_picked[:].bitcast(FP8X4), rhs_scale=e_scale[12:P, :], start=True, stop=False)
+        nc.tensor.matmul_mx(out=gate[:], lhsT=w45[0][:, 0:N].bitcast(FP8X4), lhsT_scale=w45[1][:, 0:N],
+                            rhs=nrm_codes[:].bitcast(FP8X4), rhs_scale=nrm_scale[:], start=False, stop=True)
+        sig = keep.tile([P, S], F32, name="sig")
+        nc.scalar.activation(sig[:], gate[:], ACT.Sigmoid)
+        gated = keep.tile([P, S], F32, name="gated")
+        res = keep.tile([P, S], F32, name="res")
+        halves = [slice(h * HALF, (h + 1) * HALF) for h in range(2)]
+        for cols in halves:
+            nc.vector.tensor_tensor(gated[:, cols], dot[:, cols], sig[:, cols], ALU.mult)
+        for cols in halves:
+            nc.vector.tensor_tensor(res[:, cols], gated[:, cols], skip_t[:, cols], ALU.add)
+            nc.sync.dma_start(out[:, cols], res[:, cols])

@@ -81,9 +81,9 @@ def tile_picked_ypainn_sigmoid_p_kernel(
         w2_raw = load_weight(w2, slice(0, N), "w2_raw")
         w3_raw = load_weight(w3, slice(0, N), "w3_raw")
         load_scales(3)
+        load_words(3)
         w4_raw = load_weight(w4, slice(0, N), "w4_raw")
         w5_raw = load_weight(w5, slice(0, N), "w5_raw")
-        load_words(3)
         skip_t = keep.tile([P, S], F32, name="skip_t")
         nc.sync.dma_start(skip_t[:], skip)
 
@@ -98,13 +98,16 @@ def tile_picked_ypainn_sigmoid_p_kernel(
             nc.scalar.copy(dst, src)
         nc.vector.quantize_mx(out=w1_codes[:].bitcast(FP8X4), scales=w1_scale[:], in_=w1_bf[:])
 
-        def quantize_pair(raws, grouped, name):
+        def round_pair(raws, name):
+            grouped = keep.tile([P, 2, N, PACK], BF16, name=name + "_bf", align_bytes=64)
             for i, raw in enumerate(raws):
-                dst, src = views(grouped[:, i * N * PACK : (i + 1) * N * PACK], raw[:])
-                nc.vector.tensor_copy(dst, src)
-            codes = keep.tile([P, 2 * N], U32, name=name + "_codes", align_bytes=64)
+                nc.gpsimd.tensor_scalar(grouped[:, i], raw[:].rearrange("p t c -> p c t"), 1.0, 0.0, ALU.mult, ALU.add)
+            return grouped
+
+        def quantize_pair(grouped, codes, name):
             scale = keep.tile([P, 2 * N], U8, name=name + "_scale", align_bytes=64)
-            nc.vector.quantize_mx(out=codes[:].bitcast(FP8X4), scales=scale[:], in_=grouped[:])
+            nc.vector.quantize_mx(out=codes[:].bitcast(FP8X4), scales=scale[:],
+                                  in_=grouped[:].rearrange("p a c t -> p (a c t)"))
             return codes, scale
 
         def gather_scales(c):
@@ -148,10 +151,12 @@ def tile_picked_ypainn_sigmoid_p_kernel(
             nc.scalar.activation(root[:], sums[j][:].rearrange("p t n -> p n t"), ACT.Sqrt, bias=0.05)
             roots.append(root)
 
-        w23 = quantize_pair((w2_raw, w3_raw), keep.tile([P, 2 * N * PACK], BF16, name="w23_bf", tag="win2", align_bytes=64), "w23")
         e_scale = gather_scales(3)
-        w45 = quantize_pair((w4_raw, w5_raw), first.tile([P, 2 * N * PACK], BF16, name="w45_bf", tag="scale_win3", align_bytes=64), "w45")
-        e_picked = gather_words(3, 1, first.tile([P, S], U32, name="picked_words3", tag="scale_win3", align_bytes=64))
+        w23 = quantize_pair(round_pair((w2_raw, w3_raw), "w23"),
+                            first.tile([P, 2 * N], U32, name="w23_codes", tag="scale_win3", align_bytes=64), "w23")
+        e_picked = gather_words(3, 1, keep.tile([P, S], U32, name="picked_words3", align_bytes=64))
+        w45 = quantize_pair(round_pair((w4_raw, w5_raw), "w45"),
+                            keep.tile([P, 2 * N], U32, name="w45_codes", align_bytes=64), "w45")
 
         nrm = keep.tile([P, TILES, P, PACK], BF16, name="nrm", tag="win3", align_bytes=64)
         nrm_codes = keep.tile([P, S], U32, name="nrm_codes", align_bytes=64)
@@ -177,9 +182,14 @@ def tile_picked_ypainn_sigmoid_p_kernel(
                     nc.tensor.matmul_mx(
                         out=ab[:, jj, :], lhsT=words[:, tok].bitcast(FP8X4), lhsT_scale=scale[4 * c : P, tok],
                         rhs=w23[0][:].bitcast(FP8X4), rhs_scale=w23[1][:], start=True, stop=True)
-                b_half = keep.tile([P, 2, N], F32, name="b_half%d" % step)
-                nc.scalar.activation(b_half[:], ab[:, :, N : 2 * N], ACT.Copy, scale=0.5)
-                prod = keep.tile([P, 2, N], F32, name="prod%d" % step, tag="root%d" % (step % TILES))
+                if step < 4:
+                    b_half = keep.tile([P, 2, N], F32, name="b_half%d" % step)
+                    nc.scalar.activation(b_half[:], ab[:, :, N : 2 * N], ACT.Copy, scale=0.5)
+                    prod = keep.tile([P, 2, N], F32, name="prod%d" % step, tag="root%d" % step)
+                else:
+                    b_half = keep.tile([P, 2, N], F32, name="b_half%d" % step, tag="root%d" % (step - 4))
+                    nc.vector.tensor_scalar_mul(b_half[:], ab[:, :, N : 2 * N], 0.5)
+                    prod = keep.tile([P, 2, N], F32, name="prod%d" % step)
                 nc.vector.tensor_tensor(prod[:], ab[:, :, 0:N], b_half[:], ALU.mult)
                 for jj in range(2):
                     tok = slice((2 * h + jj) * P, (2 * h + jj + 1) * P)

@@ -78,10 +78,10 @@ def tile_picked_ypainn_sigmoid_p_kernel(
         load_words(1)
         load_scales(2)
         load_words(2)
-        w2_raw = load_weight(w2, slice(0, N), "w2_raw")
-        w3_raw = load_weight(w3, slice(0, N), "w3_raw")
         load_scales(3)
         load_words(3)
+        w2_raw = load_weight(w2, slice(0, N), "w2_raw")
+        w3_raw = load_weight(w3, slice(0, N), "w3_raw")
         w4_raw = load_weight(w4, slice(0, N), "w4_raw")
         w5_raw = load_weight(w5, slice(0, N), "w5_raw")
         skip_t = keep.tile([P, S], F32, name="skip_t")
@@ -99,7 +99,7 @@ def tile_picked_ypainn_sigmoid_p_kernel(
         nc.vector.quantize_mx(out=w1_codes[:].bitcast(FP8X4), scales=w1_scale[:], in_=w1_bf[:])
 
         def round_pair(raws, name):
-            grouped = keep.tile([P, 2, N, PACK], BF16, name=name + "_bf", align_bytes=64)
+            grouped = keep.tile([P, 2, N, PACK], BF16, name=name + "_bf", tag=name + "_bf", align_bytes=64)
             for i, raw in enumerate(raws):
                 nc.gpsimd.tensor_scalar(grouped[:, i], raw[:].rearrange("p t c -> p c t"), 1.0, 0.0, ALU.mult, ALU.add)
             return grouped
@@ -123,27 +123,43 @@ def tile_picked_ypainn_sigmoid_p_kernel(
                                       word_win[c][:].bitcast(U32).indirect(offsets[:, cols]))
             return words
 
-        sums = [psum.tile([P, PACK, P], F32, name="sum%d" % j, tag="sum%d" % j) for j in range(TILES)]
+        def bank(b, shape, name):
+            return psum.tile(shape, F32, name=name, tag="bank%d" % b)
+
+        def turn_and_add(total, square, start, stop):
+            for t in range(PACK):
+                nc.tensor.matmul(out=total[:, t, :], lhsT=square[:, t, :], rhs=ident[:], is_transpose=True,
+                                 start=(start and t == 0), stop=(stop and t == PACK - 1))
+
+        work_banks = ((0, 1, 2, 3), (4, 0, 1, 2), (3, 4, 0, 1))
+        sums = [bank(5 + j, [P, PACK, P], "sum%d" % j) for j in range(TILES - 1)]
         picked = []
+        squares = []
         for c in range(3):
             scale = gather_scales(c)
-            words = gather_words(c, 1 if c == 1 else 2,
-                                 keep.tile([P, S], U32, name="picked_words%d" % c, align_bytes=64))
+            words = gather_words(c, 2, keep.tile([P, S], U32, name="picked_words%d" % c, align_bytes=64))
             picked.append((words, scale))
-            squares = []
+            row = []
             for j in range(TILES):
                 tok = slice(j * P, (j + 1) * P)
-                v = psum.tile([P, H], F32, name="v", tag="work", bufs=4)
+                v = bank(work_banks[c][j], [P, H], "v%d%d" % (c, j))
                 nc.tensor.matmul_mx(
                     out=v[:], lhsT=words[:, tok].bitcast(FP8X4), lhsT_scale=scale[4 * c : P, tok],
                     rhs=w1_codes[:].bitcast(FP8X4), rhs_scale=w1_scale[:], start=True, stop=True)
-                sq = ring.tile([P, PACK, P], F32, name="sq", tag="sq", bufs=8)
+                sq = ring.tile([P, PACK, P], F32, name="sq%d%d" % (c, j))
                 nc.scalar.activation(sq[:], v[:].rearrange("p (m t) -> p t m", t=PACK), ACT.Square)
-                squares.append(sq)
-            for j in range(TILES):
-                for t in range(PACK):
-                    nc.tensor.matmul(out=sums[j][:, t, :], lhsT=squares[j][:, t, :], rhs=ident[:], is_transpose=True,
-                                     start=(c == 0 and t == 0), stop=(c == 2 and t == PACK - 1))
+                row.append(sq)
+            squares.append(row)
+            if c < 2:
+                for j in range(TILES - 1):
+                    turn_and_add(sums[j], row[j], c == 0, False)
+        last = TILES - 1
+        sums.append(bank(work_banks[2][0], [P, PACK, P], "sum%d" % last))
+        turn_and_add(sums[0], squares[2][0], False, True)
+        turn_and_add(sums[last], squares[0][last], True, False)
+        turn_and_add(sums[last], squares[1][last], False, False)
+        for j in range(1, TILES):
+            turn_and_add(sums[j], squares[2][j], False, True)
 
         roots = []
         for j in range(TILES):
@@ -152,62 +168,67 @@ def tile_picked_ypainn_sigmoid_p_kernel(
             roots.append(root)
 
         e_scale = gather_scales(3)
-        w23 = quantize_pair(round_pair((w2_raw, w3_raw), "w23"),
-                            first.tile([P, 2 * N], U32, name="w23_codes", tag="scale_win3", align_bytes=64), "w23")
         e_picked = gather_words(3, 1, keep.tile([P, S], U32, name="picked_words3", align_bytes=64))
-        w45 = quantize_pair(round_pair((w4_raw, w5_raw), "w45"),
-                            keep.tile([P, 2 * N], U32, name="w45_codes", align_bytes=64), "w45")
+        w23_codes = keep.tile([P, 2 * N], U32, name="w23_codes", tag="win3", align_bytes=64)
+        w23 = quantize_pair(round_pair((w2_raw, w3_raw), "w23"), w23_codes, "w23")
+        w45_bf = round_pair((w4_raw, w5_raw), "w45")
 
-        nrm = keep.tile([P, TILES, P, PACK], BF16, name="nrm", tag="win3", align_bytes=64)
+        nrm = keep.tile([P, TILES, P, PACK], BF16, name="nrm", tag="w23_bf", align_bytes=64)
         nrm_codes = keep.tile([P, S], U32, name="nrm_codes", align_bytes=64)
         nrm_scale = keep.tile([P, S], U8, name="nrm_scale", align_bytes=64)
-        for h in range(2):
-            for j in (2 * h, 2 * h + 1):
-                nc.vector.tensor_tensor(nrm[:, j], roots[j][:], gain_t[:].unsqueeze(1).to_broadcast([P, P, PACK]), ALU.mult)
-            cols = slice(h * HALF, (h + 1) * HALF)
-            nc.vector.quantize_mx(out=nrm_codes[:, cols].bitcast(FP8X4), scales=nrm_scale[:, cols],
+        halves = [slice(h * HALF, (h + 1) * HALF) for h in range(2)]
+
+        def apply_gain(j):
+            nc.vector.tensor_tensor(nrm[:, j], roots[j][:],
+                                    gain_t[:].unsqueeze(1).to_broadcast([P, P, PACK]), ALU.mult)
+
+        def quantize_nrm(h):
+            nc.vector.quantize_mx(out=nrm_codes[:, halves[h]].bitcast(FP8X4), scales=nrm_scale[:, halves[h]],
                                   in_=nrm[:, 2 * h : 2 * h + 2].rearrange("p a n t -> p (a n t)"))
 
-        dot = psum.tile([P, S], F32, name="dot", tag="sum0")
-        for c in range(3):
-            words, scale = picked[c]
-            for h in range(2):
-                step = 2 * c + h
-                if step < 4:
-                    ab = psum.tile([P, 2, 2 * N], F32, name="ab", tag="work", bufs=4)
-                else:
-                    ab = psum.tile([P, 2, 2 * N], F32, name="ab", tag="sum%d" % (step - 3))
+        for j in range(3):
+            apply_gain(j)
+        quantize_nrm(0)
+        apply_gain(3)
+        w45 = quantize_pair(w45_bf, keep.tile([P, 2 * N], U32, name="w45_codes", align_bytes=64), "w45")
+        quantize_nrm(1)
+
+        gate = bank(3, [P, S], "gate")
+        nc.tensor.matmul_mx(out=gate[:], lhsT=w45[0][:, N : 2 * N].bitcast(FP8X4), lhsT_scale=w45[1][:, N : 2 * N],
+                            rhs=e_picked[:].bitcast(FP8X4), rhs_scale=e_scale[12:P, :], start=True, stop=False)
+        nc.tensor.matmul_mx(out=gate[:], lhsT=w45[0][:, 0:N].bitcast(FP8X4), lhsT_scale=w45[1][:, 0:N],
+                            rhs=nrm_codes[:].bitcast(FP8X4), rhs_scale=nrm_scale[:], start=False, stop=True)
+
+        ab_banks = ((2, 4, 0), (1, 5, 6))
+        dots = []
+        for h in range(2):
+            prods = []
+            for c in range(3):
+                words, scale = picked[c]
+                ab = bank(ab_banks[h][c], [P, 2, 2 * N], "ab%d%d" % (h, c))
                 for jj in range(2):
                     tok = slice((2 * h + jj) * P, (2 * h + jj + 1) * P)
                     nc.tensor.matmul_mx(
                         out=ab[:, jj, :], lhsT=words[:, tok].bitcast(FP8X4), lhsT_scale=scale[4 * c : P, tok],
                         rhs=w23[0][:].bitcast(FP8X4), rhs_scale=w23[1][:], start=True, stop=True)
-                if step < 4:
-                    b_half = keep.tile([P, 2, N], F32, name="b_half%d" % step)
-                    nc.scalar.activation(b_half[:], ab[:, :, N : 2 * N], ACT.Copy, scale=0.5)
-                    prod = keep.tile([P, 2, N], F32, name="prod%d" % step, tag="root%d" % step)
-                else:
-                    b_half = keep.tile([P, 2, N], F32, name="b_half%d" % step, tag="root%d" % (step - 4))
-                    nc.vector.tensor_scalar_mul(b_half[:], ab[:, :, N : 2 * N], 0.5)
-                    prod = keep.tile([P, 2, N], F32, name="prod%d" % step)
+                b_half = keep.tile([P, 2, N], F32, name="b_half%d%d" % (h, c))
+                nc.scalar.activation(b_half[:], ab[:, :, N : 2 * N], ACT.Copy, scale=0.5)
+                prod = keep.tile([P, 2, N], F32, name="prod%d%d" % (h, c))
                 nc.vector.tensor_tensor(prod[:], ab[:, :, 0:N], b_half[:], ALU.mult)
+                prods.append(prod)
+            dot = bank((7, 2)[h], [P, HALF], "dot%d" % h)
+            for c in range(3):
                 for jj in range(2):
-                    tok = slice((2 * h + jj) * P, (2 * h + jj + 1) * P)
-                    nc.tensor.matmul(out=dot[:, tok], lhsT=prod[:, jj, :], rhs=ident[:], is_transpose=True,
-                                     start=(step == 0 and jj == 0), stop=(step == 5 and jj == 1))
+                    nc.tensor.matmul(out=dot[:, jj * P : (jj + 1) * P], lhsT=prods[c][:, jj, :], rhs=ident[:],
+                                     is_transpose=True, start=(c == 0 and jj == 0), stop=(c == 2 and jj == 1))
+            dots.append(dot)
 
-        gate = psum.tile([P, S], F32, name="gate", tag="sum3")
-        nc.tensor.matmul_mx(out=gate[:], lhsT=w45[0][:, N : 2 * N].bitcast(FP8X4), lhsT_scale=w45[1][:, N : 2 * N],
-                            rhs=e_picked[:].bitcast(FP8X4), rhs_scale=e_scale[12:P, :], start=True, stop=False)
-        nc.tensor.matmul_mx(out=gate[:], lhsT=w45[0][:, 0:N].bitcast(FP8X4), lhsT_scale=w45[1][:, 0:N],
-                            rhs=nrm_codes[:].bitcast(FP8X4), rhs_scale=nrm_scale[:], start=False, stop=True)
         sig = keep.tile([P, S], F32, name="sig")
         nc.scalar.activation(sig[:], gate[:], ACT.Sigmoid)
         gated = keep.tile([P, S], F32, name="gated")
         res = keep.tile([P, S], F32, name="res")
-        halves = [slice(h * HALF, (h + 1) * HALF) for h in range(2)]
-        for cols in halves:
-            nc.vector.tensor_tensor(gated[:, cols], dot[:, cols], sig[:, cols], ALU.mult)
+        for h, cols in enumerate(halves):
+            nc.vector.tensor_tensor(gated[:, cols], dots[h][:], sig[:, cols], ALU.mult)
         for cols in halves:
             nc.vector.tensor_tensor(res[:, cols], gated[:, cols], skip_t[:, cols], ALU.add)
             nc.sync.dma_start(out[:, cols], res[:, cols])

@@ -38,11 +38,11 @@ def tile_picked_ypainn_sigmoid_p_kernel(
         nc.sync.dma_start(offsets[:], offs)
 
         scale_win = [first.tile([P, T], U8, name="scale_win%d" % c, tag="scale_win%d" % c, align_bytes=64) for c in range(4)]
-        for c in range(4):
-            (nc.vector if c % 2 == 0 else nc.gpsimd).memset(scale_win[c][:].bitcast(I32), 0)
+        for c in (0, 2, 1, 3):
+            nc.vector.memset(scale_win[c][:].bitcast(I32), 0)
 
         ident = first.tile([P, P], F32, name="ident")
-        w1_raw = [first.tile([P, PACK, 256], F32, name="w1_raw%d" % h) for h in range(2)]
+        w1_raw = first.tile([P, PACK, H], F32, name="w1_raw")
         w1_bf = first.tile([P, H * PACK], BF16, name="w1_bf", align_bytes=64)
         with tc.tile_pool(name="warm", bufs=1) as warm_pool:
             warm = warm_pool.tile([P, 2], F32, name="warm")
@@ -54,7 +54,7 @@ def tile_picked_ypainn_sigmoid_p_kernel(
 
         def load_scales(c):
             for r in range(4):
-                nc.sync.dma_start(
+                (nc.gpsimd if c == 2 else nc.sync).dma_start(
                     scale_win[c][4 * c + r : P : 32, :].bitcast(I32),
                     scales_in[c][0, r:16:4, :].bitcast(I32),
                 )
@@ -68,22 +68,22 @@ def tile_picked_ypainn_sigmoid_p_kernel(
             nc.sync.dma_start(raw[:], w.rearrange("(p j) c -> p j c", j=PACK)[:, :, cols])
             return raw
 
-        for h in range(2):
-            nc.sync.dma_start(w1_raw[h][:], w1.rearrange("(p j) c -> p j c", j=PACK)[:, :, h * 256 : (h + 1) * 256])
+        nc.sync.dma_start(w1_raw[:], w1.rearrange("(p j) c -> p j c", j=PACK))
         load_scales(0)
         load_words(0)
-        gain_t = keep.tile([P, PACK], F32, name="gain_t")
-        nc.sync.dma_start(gain_t[:], gain.rearrange("(p j) o -> p (j o)", j=PACK))
         load_scales(1)
         load_words(1)
         load_scales(2)
         load_words(2)
         load_scales(3)
-        load_words(3)
+        gain_t = keep.tile([P, PACK], F32, name="gain_t")
+        nc.sync.dma_start(gain_t[:], gain.rearrange("(p j) o -> p (j o)", j=PACK))
         w2_raw = load_weight(w2, slice(0, N), "w2_raw")
         w3_raw = load_weight(w3, slice(0, N), "w3_raw")
-        w4_raw = load_weight(w4, slice(0, N), "w4_raw")
-        w5_raw = load_weight(w5, slice(0, N), "w5_raw")
+        w45_raw = keep.tile([P, 2, PACK, N], F32, name="w45_raw")
+        for i, w in enumerate((w4, w5)):
+            nc.sync.dma_start(w45_raw[:, i], w.rearrange("(p j) c -> p j c", j=PACK))
+        load_words(3)
         skip_t = keep.tile([P, S], F32, name="skip_t")
         nc.sync.dma_start(skip_t[:], skip)
 
@@ -93,9 +93,8 @@ def tile_picked_ypainn_sigmoid_p_kernel(
 
         w1_codes = first.tile([P, H], U32, name="w1_codes", tag="scale_win0", align_bytes=64)
         w1_scale = keep.tile([P, H], U8, name="w1_scale", align_bytes=64)
-        for h in range(2):
-            dst, src = views(w1_bf[:, h * 256 * PACK : (h + 1) * 256 * PACK], w1_raw[h][:])
-            nc.scalar.copy(dst, src)
+        for h, copy in enumerate((nc.scalar.copy, nc.vector.tensor_copy)):
+            copy(*views(w1_bf[:, h * 256 * PACK : (h + 1) * 256 * PACK], w1_raw[:, :, h * 256 : (h + 1) * 256]))
         nc.vector.quantize_mx(out=w1_codes[:].bitcast(FP8X4), scales=w1_scale[:], in_=w1_bf[:])
 
         def round_pair(raws, name):
@@ -111,7 +110,7 @@ def tile_picked_ypainn_sigmoid_p_kernel(
             return codes, scale
 
         def gather_scales(c):
-            scale = keep.tile([P, S], U8, name="picked_scale%d" % c, tag="win%d" % (c - 1), align_bytes=64)
+            scale = keep.tile([P, S], U8, name="picked_scale%d" % c, tag="win1" if c == 2 else "picked_scale%d" % c, align_bytes=64)
             nc.vector.tensor_copy(scale[:], scale_win[c][:].indirect(offsets[:]))
             return scale
 
@@ -132,46 +131,58 @@ def tile_picked_ypainn_sigmoid_p_kernel(
                                  start=(start and t == 0), stop=(stop and t == PACK - 1))
 
         work_banks = ((0, 1, 2, 3), (4, 0, 1, 2), (3, 4, 0, 1))
-        sums = [bank(5 + j, [P, PACK, P], "sum%d" % j) for j in range(TILES - 1)]
+        last = TILES - 1
+        sums = [bank(5 + j, [P, PACK, P], "sum%d" % j) for j in range(last)]
         picked = []
-        squares = []
+        squares = {}
+        roots = []
+
+        def square(c, j):
+            words, scale = picked[c]
+            tok = slice(j * P, (j + 1) * P)
+            v = bank(work_banks[c][j], [P, H], "v%d%d" % (c, j))
+            nc.tensor.matmul_mx(
+                out=v[:], lhsT=words[:, tok].bitcast(FP8X4), lhsT_scale=scale[4 * c : P, tok],
+                rhs=w1_codes[:].bitcast(FP8X4), rhs_scale=w1_scale[:], start=True, stop=True)
+            sq = ring.tile([P, PACK, P], F32, name="sq%d%d" % (c, j))
+            squares[c, j] = sq
+            return lambda: nc.scalar.activation(sq[:], v[:].rearrange("p (m t) -> p t m", t=PACK), ACT.Square)
+
+        def root_of(j):
+            root = keep.tile([P, P, PACK], F32, name="root%d" % j)
+            nc.scalar.activation(root[:], sums[j][:].rearrange("p t n -> p n t"), ACT.Sqrt, bias=0.05)
+            roots.append(root)
+
         for c in range(3):
             scale = gather_scales(c)
             words = gather_words(c, 2, keep.tile([P, S], U32, name="picked_words%d" % c, align_bytes=64))
             picked.append((words, scale))
-            row = []
-            for j in range(TILES):
-                tok = slice(j * P, (j + 1) * P)
-                v = bank(work_banks[c][j], [P, H], "v%d%d" % (c, j))
-                nc.tensor.matmul_mx(
-                    out=v[:], lhsT=words[:, tok].bitcast(FP8X4), lhsT_scale=scale[4 * c : P, tok],
-                    rhs=w1_codes[:].bitcast(FP8X4), rhs_scale=w1_scale[:], start=True, stop=True)
-                sq = ring.tile([P, PACK, P], F32, name="sq%d%d" % (c, j))
-                nc.scalar.activation(sq[:], v[:].rearrange("p (m t) -> p t m", t=PACK), ACT.Square)
-                row.append(sq)
-            squares.append(row)
+            pending = [square(c, j) for j in range(TILES)]
             if c < 2:
-                for j in range(TILES - 1):
-                    turn_and_add(sums[j], row[j], c == 0, False)
-        last = TILES - 1
+                for take_square in pending:
+                    take_square()
+                for j in range(last):
+                    turn_and_add(sums[j], squares[c, j], c == 0, False)
+        for j in range(2):
+            pending[j]()
+            turn_and_add(sums[j], squares[2, j], False, True)
         sums.append(bank(work_banks[2][0], [P, PACK, P], "sum%d" % last))
-        turn_and_add(sums[0], squares[2][0], False, True)
-        turn_and_add(sums[last], squares[0][last], True, False)
-        turn_and_add(sums[last], squares[1][last], False, False)
-        for j in range(1, TILES):
-            turn_and_add(sums[j], squares[2][j], False, True)
-
-        roots = []
-        for j in range(TILES):
-            root = keep.tile([P, P, PACK], F32, name="root%d" % j, tag="root%d" % j)
-            nc.scalar.activation(root[:], sums[j][:].rearrange("p t n -> p n t"), ACT.Sqrt, bias=0.05)
-            roots.append(root)
+        turn_and_add(sums[last], squares[0, last], True, False)
+        turn_and_add(sums[last], squares[1, last], False, False)
+        for j in range(2):
+            root_of(j)
+        for j in range(2, TILES):
+            pending[j]()
+            turn_and_add(sums[j], squares[2, j], False, True)
+        for j in range(2, TILES):
+            root_of(j)
 
         e_scale = gather_scales(3)
-        e_picked = gather_words(3, 1, keep.tile([P, S], U32, name="picked_words3", align_bytes=64))
-        w23_codes = keep.tile([P, 2 * N], U32, name="w23_codes", tag="win3", align_bytes=64)
+        w23_codes = keep.tile([P, 2 * N], U32, name="w23_codes", align_bytes=64)
         w23 = quantize_pair(round_pair((w2_raw, w3_raw), "w23"), w23_codes, "w23")
-        w45_bf = round_pair((w4_raw, w5_raw), "w45")
+
+        w45_bf = keep.tile([P, 2, N, PACK], BF16, name="w45_bf", tag="w45_bf", align_bytes=64)
+        nc.vector.tensor_copy(w45_bf[:], w45_raw[:].rearrange("p a t c -> p a c t"))
 
         nrm = keep.tile([P, TILES, P, PACK], BF16, name="nrm", tag="w23_bf", align_bytes=64)
         nrm_codes = keep.tile([P, S], U32, name="nrm_codes", align_bytes=64)
@@ -186,11 +197,13 @@ def tile_picked_ypainn_sigmoid_p_kernel(
             nc.vector.quantize_mx(out=nrm_codes[:, halves[h]].bitcast(FP8X4), scales=nrm_scale[:, halves[h]],
                                   in_=nrm[:, 2 * h : 2 * h + 2].rearrange("p a n t -> p (a n t)"))
 
-        for j in range(3):
-            apply_gain(j)
+        apply_gain(0)
+        w45 = quantize_pair(w45_bf, keep.tile([P, 2 * N], U32, name="w45_codes", align_bytes=64), "w45")
+        apply_gain(1)
+        apply_gain(2)
         quantize_nrm(0)
         apply_gain(3)
-        w45 = quantize_pair(w45_bf, keep.tile([P, 2 * N], U32, name="w45_codes", align_bytes=64), "w45")
+        e_picked = gather_words(3, 1, keep.tile([P, S], U32, name="picked_words3", align_bytes=64))
         quantize_nrm(1)
 
         gate = bank(3, [P, S], "gate")
@@ -199,10 +212,10 @@ def tile_picked_ypainn_sigmoid_p_kernel(
         nc.tensor.matmul_mx(out=gate[:], lhsT=w45[0][:, 0:N].bitcast(FP8X4), lhsT_scale=w45[1][:, 0:N],
                             rhs=nrm_codes[:].bitcast(FP8X4), rhs_scale=nrm_scale[:], start=False, stop=True)
 
-        ab_banks = ((2, 4, 0), (1, 5, 6))
+        ab_banks = ((2, 4, 5), (6, 0, 1))
         dots = []
+        products = keep.tile([P, 2, 3, 2, N], F32, name="products")
         for h in range(2):
-            prods = []
             for c in range(3):
                 words, scale = picked[c]
                 ab = bank(ab_banks[h][c], [P, 2, 2 * N], "ab%d%d" % (h, c))
@@ -213,18 +226,17 @@ def tile_picked_ypainn_sigmoid_p_kernel(
                         rhs=w23[0][:].bitcast(FP8X4), rhs_scale=w23[1][:], start=True, stop=True)
                 b_half = keep.tile([P, 2, N], F32, name="b_half%d%d" % (h, c))
                 nc.scalar.activation(b_half[:], ab[:, :, N : 2 * N], ACT.Copy, scale=0.5)
-                prod = keep.tile([P, 2, N], F32, name="prod%d%d" % (h, c))
-                nc.vector.tensor_tensor(prod[:], ab[:, :, 0:N], b_half[:], ALU.mult)
-                prods.append(prod)
+                nc.vector.tensor_tensor(products[:, h, c], ab[:, :, 0:N], b_half[:], ALU.mult)
             dot = bank((7, 2)[h], [P, HALF], "dot%d" % h)
             for c in range(3):
                 for jj in range(2):
-                    nc.tensor.matmul(out=dot[:, jj * P : (jj + 1) * P], lhsT=prods[c][:, jj, :], rhs=ident[:],
+                    nc.tensor.matmul(out=dot[:, jj * P : (jj + 1) * P], lhsT=products[:, h, c, jj, :], rhs=ident[:],
                                      is_transpose=True, start=(c == 0 and jj == 0), stop=(c == 2 and jj == 1))
             dots.append(dot)
 
         sig = keep.tile([P, S], F32, name="sig")
-        nc.scalar.activation(sig[:], gate[:], ACT.Sigmoid)
+        for cols in halves:
+            nc.scalar.activation(sig[:, cols], gate[:, cols], ACT.Sigmoid)
         gated = keep.tile([P, S], F32, name="gated")
         res = keep.tile([P, S], F32, name="res")
         for h, cols in enumerate(halves):

@@ -54,7 +54,7 @@ def tile_picked_ypainn_sigmoid_p_kernel(
 
         def load_scales(c):
             for r in range(4):
-                (nc.gpsimd if c == 2 else nc.sync).dma_start(
+                (nc.gpsimd if c >= 2 else nc.sync).dma_start(
                     scale_win[c][4 * c + r : P : 32, :].bitcast(I32),
                     scales_in[c][0, r:16:4, :].bitcast(I32),
                 )
@@ -110,7 +110,7 @@ def tile_picked_ypainn_sigmoid_p_kernel(
             return codes, scale
 
         def gather_scales(c):
-            scale = keep.tile([P, S], U8, name="picked_scale%d" % c, tag="win1" if c == 2 else "picked_scale%d" % c, align_bytes=64)
+            scale = keep.tile([P, S], U8, name="picked_scale%d" % c, tag="win%d" % (c - 1) if c >= 2 else "picked_scale%d" % c, align_bytes=64)
             nc.vector.tensor_copy(scale[:], scale_win[c][:].indirect(offsets[:]))
             return scale
 
@@ -130,9 +130,9 @@ def tile_picked_ypainn_sigmoid_p_kernel(
                 nc.tensor.matmul(out=total[:, t, :], lhsT=square[:, t, :], rhs=ident[:], is_transpose=True,
                                  start=(start and t == 0), stop=(stop and t == PACK - 1))
 
-        work_banks = ((0, 1, 2, 3), (4, 0, 1, 2), (3, 4, 0, 1))
-        last = TILES - 1
-        sums = [bank(5 + j, [P, PACK, P], "sum%d" % j) for j in range(last)]
+        work_banks = ((0, 1, 2, 3), (4, 5, 6, 0), (1, 2, 3, 6))
+        sum_banks = (7, 4, 5, 1)
+        sums = {}
         picked = []
         squares = {}
         roots = []
@@ -153,6 +153,11 @@ def tile_picked_ypainn_sigmoid_p_kernel(
             nc.scalar.activation(root[:], sums[j][:].rearrange("p t n -> p n t"), ACT.Sqrt, bias=0.05)
             roots.append(root)
 
+        def add_square(c, j):
+            if c == 0:
+                sums[j] = bank(sum_banks[j], [P, PACK, P], "sum%d" % j)
+            turn_and_add(sums[j], squares[c, j], c == 0, c == 2)
+
         for c in range(3):
             scale = gather_scales(c)
             words = gather_words(c, 2, keep.tile([P, S], U32, name="picked_words%d" % c, align_bytes=64))
@@ -161,19 +166,21 @@ def tile_picked_ypainn_sigmoid_p_kernel(
             if c < 2:
                 for take_square in pending:
                     take_square()
-                for j in range(last):
-                    turn_and_add(sums[j], squares[c, j], c == 0, False)
+            if c == 0:
+                add_square(0, 0)
+            if c == 1:
+                for step in ((0, 1), (1, 0), (1, 1), (0, 2)):
+                    add_square(*step)
         for j in range(2):
             pending[j]()
-            turn_and_add(sums[j], squares[2, j], False, True)
-        sums.append(bank(work_banks[2][0], [P, PACK, P], "sum%d" % last))
-        turn_and_add(sums[last], squares[0, last], True, False)
-        turn_and_add(sums[last], squares[1, last], False, False)
+            add_square(2, j)
+        for step in ((1, 2), (0, 3), (1, 3)):
+            add_square(*step)
         for j in range(2):
             root_of(j)
         for j in range(2, TILES):
             pending[j]()
-            turn_and_add(sums[j], squares[2, j], False, True)
+            add_square(2, j)
         for j in range(2, TILES):
             root_of(j)
 
@@ -206,13 +213,13 @@ def tile_picked_ypainn_sigmoid_p_kernel(
         e_picked = gather_words(3, 1, keep.tile([P, S], U32, name="picked_words3", align_bytes=64))
         quantize_nrm(1)
 
-        gate = bank(3, [P, S], "gate")
+        gate = bank(1, [P, S], "gate")
         nc.tensor.matmul_mx(out=gate[:], lhsT=w45[0][:, N : 2 * N].bitcast(FP8X4), lhsT_scale=w45[1][:, N : 2 * N],
                             rhs=e_picked[:].bitcast(FP8X4), rhs_scale=e_scale[12:P, :], start=True, stop=False)
         nc.tensor.matmul_mx(out=gate[:], lhsT=w45[0][:, 0:N].bitcast(FP8X4), lhsT_scale=w45[1][:, 0:N],
                             rhs=nrm_codes[:].bitcast(FP8X4), rhs_scale=nrm_scale[:], start=False, stop=True)
 
-        ab_banks = ((2, 4, 5), (6, 0, 1))
+        ab_banks = ((0, 2, 7), (4, 3, 6))
         dots = []
         products = keep.tile([P, 2, 3, 2, N], F32, name="products")
         for h in range(2):
@@ -227,7 +234,7 @@ def tile_picked_ypainn_sigmoid_p_kernel(
                 b_half = keep.tile([P, 2, N], F32, name="b_half%d%d" % (h, c))
                 nc.scalar.activation(b_half[:], ab[:, :, N : 2 * N], ACT.Copy, scale=0.5)
                 nc.vector.tensor_tensor(products[:, h, c], ab[:, :, 0:N], b_half[:], ALU.mult)
-            dot = bank((7, 2)[h], [P, HALF], "dot%d" % h)
+            dot = bank((5, 0)[h], [P, HALF], "dot%d" % h)
             for c in range(3):
                 for jj in range(2):
                     nc.tensor.matmul(out=dot[:, jj * P : (jj + 1) * P], lhsT=products[:, h, c, jj, :], rhs=ident[:],

@@ -1,3 +1,4 @@
+import math
 from contextlib import ExitStack
 
 import concourse.mybir as mybir
@@ -18,7 +19,11 @@ PACK = 4
 K, T, S, H, N = 512, 2048, 512, 512, 128
 HALF = S // 2
 TILES = S // P
+EPS = 0.05
+W1_SCALAR_SHARE = 320
 FLOPS = 2 * K * S * (3 * H + 7 * N) + 2 * H * S * N
+X, Y, Z, E = range(4)
+WINDOW_BYTES = 4 * T
 
 
 def tile_picked_ypainn_sigmoid_p_kernel(
@@ -28,226 +33,226 @@ def tile_picked_ypainn_sigmoid_p_kernel(
     nc = tc.nc
     words_in = (x_words, g_words, d_words, e_words)
     scales_in = (x_scales, g_scales, d_scales, e_scales)
+    halves = [slice(h * HALF, (h + 1) * HALF) for h in range(2)]
+    tiles = [slice(j * P, (j + 1) * P) for j in range(TILES)]
 
     with ExitStack() as ctx:
-        first = ctx.enter_context(tc.tile_pool(name="first", bufs=1))
-        ring = ctx.enter_context(tc.tile_pool(name="ring", bufs=1))
+        keep = ctx.enter_context(tc.tile_pool(name="keep", bufs=1))
         psum = ctx.enter_context(tc.psum_pool(name="psum", bufs=1))
 
-        offsets = first.tile([P, S // 16], U16, name="offsets")
-        nc.sync.dma_start(offsets[:], offs)
-
-        scale_win = [first.tile([P, T], U8, name="scale_win%d" % c, tag="scale_win%d" % c, align_bytes=64) for c in range(4)]
-        for c in (0, 2, 1, 3):
-            nc.vector.memset(scale_win[c][:].bitcast(I32), 0)
-
-        ident = first.tile([P, P], F32, name="ident")
-        w1_raw = first.tile([P, PACK, H], F32, name="w1_raw")
-        w1_bf = first.tile([P, H * PACK], BF16, name="w1_bf", align_bytes=64)
-        with tc.tile_pool(name="warm", bufs=1) as warm_pool:
-            warm = warm_pool.tile([P, 2], F32, name="warm")
-            nc.gpsimd.memset(warm[:, 0:1], 1.0)
-            nc.scalar.activation(warm[:, 1:2], warm[:, 0:1], ACT.Sqrt)
-        make_identity(nc, ident[:])
-        keep = ctx.enter_context(tc.tile_pool(name="keep", bufs=1))
-        word_win = [keep.tile([P, T], I32, name="word_win%d" % c, tag="win%d" % c, align_bytes=64) for c in range(4)]
-
-        def load_scales(c):
-            for r in range(4):
-                (nc.gpsimd if c >= 2 else nc.sync).dma_start(
-                    scale_win[c][4 * c + r : P : 32, :].bitcast(I32),
-                    scales_in[c][0, r:16:4, :].bitcast(I32),
-                )
-
-        def load_words(c):
-            nc.sync.dma_start(word_win[c][:], words_in[c][0].rearrange("p n t -> p (n t)").bitcast(I32))
-
-        def load_weight(w, cols, name):
-            width = cols.stop - cols.start
-            raw = keep.tile([P, PACK, width], F32, name=name)
-            nc.sync.dma_start(raw[:], w.rearrange("(p j) c -> p j c", j=PACK)[:, :, cols])
-            return raw
-
-        nc.sync.dma_start(w1_raw[:], w1.rearrange("(p j) c -> p j c", j=PACK))
-        load_scales(0)
-        load_words(0)
-        load_scales(1)
-        load_words(1)
-        load_scales(2)
-        load_words(2)
-        load_scales(3)
-        gain_t = keep.tile([P, PACK], F32, name="gain_t")
-        nc.sync.dma_start(gain_t[:], gain.rearrange("(p j) o -> p (j o)", j=PACK))
-        w2_raw = load_weight(w2, slice(0, N), "w2_raw")
-        w3_raw = load_weight(w3, slice(0, N), "w3_raw")
-        w45_raw = keep.tile([P, 2, PACK, N], F32, name="w45_raw")
-        for i, w in enumerate((w4, w5)):
-            nc.sync.dma_start(w45_raw[:, i], w.rearrange("(p j) c -> p j c", j=PACK))
-        load_words(3)
-        skip_t = keep.tile([P, S], F32, name="skip_t")
-        nc.sync.dma_start(skip_t[:], skip)
-
-        def views(grouped, raw):
-            return (grouped.rearrange("p (c i t) -> p c t i", i=4, t=PACK),
-                    raw.rearrange("p t (c i) -> p c t i", i=4))
-
-        w1_codes = first.tile([P, H], U32, name="w1_codes", tag="scale_win0", align_bytes=64)
-        w1_scale = keep.tile([P, H], U8, name="w1_scale", align_bytes=64)
-        for h, copy in enumerate((nc.scalar.copy, nc.vector.tensor_copy)):
-            copy(*views(w1_bf[:, h * 256 * PACK : (h + 1) * 256 * PACK], w1_raw[:, :, h * 256 : (h + 1) * 256]))
-        nc.vector.quantize_mx(out=w1_codes[:].bitcast(FP8X4), scales=w1_scale[:], in_=w1_bf[:])
-
-        def round_pair(raws, name):
-            grouped = keep.tile([P, 2, N, PACK], BF16, name=name + "_bf", tag=name + "_bf", align_bytes=64)
-            for i, raw in enumerate(raws):
-                nc.gpsimd.tensor_scalar(grouped[:, i], raw[:].rearrange("p t c -> p c t"), 1.0, 0.0, ALU.mult, ALU.add)
-            return grouped
-
-        def quantize_pair(grouped, codes, name):
-            scale = keep.tile([P, 2 * N], U8, name=name + "_scale", align_bytes=64)
-            nc.vector.quantize_mx(out=codes[:].bitcast(FP8X4), scales=scale[:],
-                                  in_=grouped[:].rearrange("p a c t -> p (a c t)"))
-            return codes, scale
-
-        def gather_scales(c):
-            scale = keep.tile([P, S], U8, name="picked_scale%d" % c, tag="win%d" % (c - 1) if c >= 2 else "picked_scale%d" % c, align_bytes=64)
-            nc.vector.tensor_copy(scale[:], scale_win[c][:].indirect(offsets[:]))
-            return scale
-
-        def gather_words(c, pieces, words):
-            width = S // pieces
-            for h in range(pieces):
-                cols = slice(h * width // 16, (h + 1) * width // 16)
-                nc.vector.tensor_copy(words[:, h * width : (h + 1) * width],
-                                      word_win[c][:].bitcast(U32).indirect(offsets[:, cols]))
-            return words
+        def sbuf(shape, dtype, name, tag=None):
+            return keep.tile(shape, dtype, name=name, tag=tag or name, align_bytes=64)
 
         def bank(b, shape, name):
             return psum.tile(shape, F32, name=name, tag="bank%d" % b)
 
-        def turn_and_add(total, square, start, stop):
+        offsets = keep.tile([P, S // 16], U16, name="offsets")
+        nc.sync.dma_start(offsets[:], offs)
+
+        scale_win = [sbuf([P, T], U8, "scale_win%d" % c) for c in range(4)]
+        for c in (X, Z, Y, E):
+            nc.vector.memset(scale_win[c][:].bitcast(I32), 0)
+        shared = ctx.enter_context(tc.tile_pool(name="shared", bufs=1))
+        word_win = [shared.tile([P, T], I32, name="word_win%d" % c, offset=c * WINDOW_BYTES, align_bytes=64) for c in range(4)]
+
+        def after_gather_of(c, at, shape, dtype, name):
+            return shared.tile(shape, dtype, name=name, offset=c * WINDOW_BYTES + at, align_bytes=64)
+
+        one = sbuf([P, 1], F32, "one")
+        nc.gpsimd.memset(one[:], 1.0)
+        warm = sbuf([P, 1], F32, "warm")
+        nc.scalar.activation(warm[:], one[:], ACT.Sqrt)
+        ident = sbuf([P, P], F32, "ident")
+        make_identity(nc, ident[:])
+
+        def load_scales(c, queue):
+            for r in range(4):
+                queue.dma_start(scale_win[c][4 * c + r : P : 32, :].bitcast(I32),
+                                scales_in[c][0, r:16:4, :].bitcast(I32))
+
+        def load_words(c):
+            nc.sync.dma_start(word_win[c][:], words_in[c][0].rearrange("p n t -> p (n t)").bitcast(I32))
+
+        def load_weight(raw, w):
+            nc.sync.dma_start(raw, w.rearrange("(p j) c -> p j c", j=PACK))
+
+        w1_raw = sbuf([P, PACK, H], F32, "w1_raw")
+        w23_raw = sbuf([P, 2, PACK, N], F32, "w23_raw")
+        w4_raw = sbuf([P, PACK, N], F32, "w4_raw")
+        w5_raw = sbuf([P, PACK, N], F32, "w5_raw")
+        gain_t = sbuf([P, PACK], F32, "gain_t")
+        skip_t = sbuf([P, S], F32, "skip_t")
+
+        load_weight(w1_raw[:], w1)
+        load_scales(X, nc.sync)
+        load_words(X)
+        nc.sync.dma_start(gain_t[:], gain.rearrange("(p j) o -> p (j o)", j=PACK))
+        load_scales(Y, nc.sync)
+        load_words(Y)
+        load_words(Z)
+        load_weight(w23_raw[:, 0], w2)
+        load_weight(w23_raw[:, 1], w3)
+        load_weight(w4_raw[:], w4)
+        load_weight(w5_raw[:], w5)
+        load_words(E)
+        nc.sync.dma_start(skip_t[:], skip)
+        load_scales(Z, nc.gpsimd)
+        load_scales(E, nc.gpsimd)
+
+        def interleave(copy, grouped, planes):
+            copy(grouped.rearrange("p (c i) t -> p c t i", i=4), planes.rearrange("p t (c i) -> p c t i", i=4))
+
+        w1_bf = sbuf([P, H, PACK], BF16, "w1_bf")
+        interleave(nc.scalar.copy, w1_bf[:, :W1_SCALAR_SHARE, :], w1_raw[:, :, :W1_SCALAR_SHARE])
+        interleave(nc.vector.tensor_copy, w1_bf[:, W1_SCALAR_SHARE:, :], w1_raw[:, :, W1_SCALAR_SHARE:])
+
+        def quantize(values, width, name, tag=None):
+            codes = sbuf([P, width], U32, name + "_codes", tag)
+            scale = sbuf([P, width], U8, name + "_scale")
+            nc.vector.quantize_mx(out=codes[:].bitcast(FP8X4), scales=scale[:], in_=values)
+            return codes, scale
+
+        def gather_scales(c, scale):
+            nc.vector.tensor_copy(scale[:], scale_win[c][:].indirect(offsets[:]))
+            return scale
+
+        def gather_words(c, pieces):
+            words = sbuf([P, S], U32, "picked_words%d" % c)
+            width = S // pieces
+            for h in range(pieces):
+                nc.vector.tensor_copy(words[:, h * width : (h + 1) * width],
+                                      word_win[c][:].bitcast(U32).indirect(offsets[:, h * width // 16 : (h + 1) * width // 16]))
+            return words
+
+        def product(result, lhs, lhs_cols, rhs, rhs_cols, start=True, stop=True):
+            nc.tensor.matmul_mx(out=result, lhsT=lhs[0][:, lhs_cols].bitcast(FP8X4), lhsT_scale=lhs[1][:, lhs_cols],
+                                rhs=rhs[0][:, rhs_cols].bitcast(FP8X4), rhs_scale=rhs[1][:, rhs_cols],
+                                start=start, stop=stop)
+
+        x_scale = gather_scales(X, sbuf([P, S], U8, "picked_scale_x"))
+        w1_mx = quantize(w1_bf[:].rearrange("p c t -> p (c t)"), H, "w1", "scale_win%d" % X)
+
+        gain_sq = sbuf([P, PACK], F32, "gain_sq")
+        gain_eps = sbuf([P, PACK], F32, "gain_eps")
+        gain_sign = sbuf([P, PACK], F32, "gain_sign")
+        nc.scalar.activation(gain_sq[:], gain_t[:], ACT.Square)
+        nc.scalar.activation(gain_eps[:], gain_t[:], ACT.Square, scale=math.sqrt(EPS))
+        nc.scalar.activation(gain_sign[:], gain_t[:], ACT.Sign)
+
+        def squares_of(c, picked, banks):
+            squares = []
+            for j in range(TILES):
+                v = bank(banks[j], [P, H], "v%d%d" % (c, j))
+                product(v[:], picked, tiles[j], w1_mx, slice(0, H))
+                sq = sbuf([P, PACK, P], F32, "sq%d%d" % (c, j))
+                nc.scalar.activation(sq[:], v[:].rearrange("p (m t) -> p t m", t=PACK), ACT.Square)
+                squares.append(sq)
+            return squares
+
+        x_mx = (gather_words(X, 2), x_scale[4 * X : P])
+        x_squares = squares_of(X, x_mx, (0, 1, 2, 3))
+        y_scale = gather_scales(Y, sbuf([P, S], U8, "picked_scale_y"))
+        y_mx = (gather_words(Y, 2), y_scale[4 * Y : P])
+        y_squares = squares_of(Y, y_mx, (4, 5, 0, 1))
+        z_scale = gather_scales(Z, after_gather_of(Y, 0, [P, S], U8, "picked_scale_z"))
+        z_mx = (gather_words(Z, 2), z_scale[4 * Z : P])
+        e_scale = gather_scales(E, after_gather_of(Z, 0, [P, S], U8, "picked_scale_e"))
+        z_squares = squares_of(Z, z_mx, (2, 3, 0, 1))
+
+        sum_banks = ((6, 7), (4, 5))
+        lengths = [sbuf([P, PACK, HALF], BF16, "lengths%d" % h) for h in range(2)]
+        nrm_mx = (sbuf([P, S], U32, "nrm_codes"), sbuf([P, S], U8, "nrm_scale"))
+
+        def lengths_of(h):
+            sums = [bank(sum_banks[h][u], [P, 2, HALF], "sum%d%d" % (h, u)) for u in range(2)]
+            for c, squares in enumerate((x_squares, y_squares, z_squares)):
+                for jj in range(2):
+                    for t in range(PACK):
+                        nc.tensor.matmul(out=sums[t // 2][:, t % 2, tiles[jj]], lhsT=squares[2 * h + jj][:, t, :],
+                                         rhs=ident[:], is_transpose=True,
+                                         start=(c == X and jj == 0 and t % 2 == 0), stop=(c == Z and jj == 1 and t % 2 == 1))
             for t in range(PACK):
-                nc.tensor.matmul(out=total[:, t, :], lhsT=square[:, t, :], rhs=ident[:], is_transpose=True,
-                                 start=(start and t == 0), stop=(stop and t == PACK - 1))
-
-        work_banks = ((0, 1, 2, 3), (4, 5, 6, 0), (1, 2, 3, 6))
-        sum_banks = (7, 4, 5, 1)
-        sums = {}
-        picked = []
-        squares = {}
-        roots = []
-
-        def square(c, j):
-            words, scale = picked[c]
-            tok = slice(j * P, (j + 1) * P)
-            v = bank(work_banks[c][j], [P, H], "v%d%d" % (c, j))
-            nc.tensor.matmul_mx(
-                out=v[:], lhsT=words[:, tok].bitcast(FP8X4), lhsT_scale=scale[4 * c : P, tok],
-                rhs=w1_codes[:].bitcast(FP8X4), rhs_scale=w1_scale[:], start=True, stop=True)
-            sq = ring.tile([P, PACK, P], F32, name="sq%d%d" % (c, j))
-            squares[c, j] = sq
-            return lambda: nc.scalar.activation(sq[:], v[:].rearrange("p (m t) -> p t m", t=PACK), ACT.Square)
-
-        def root_of(j):
-            root = keep.tile([P, P, PACK], F32, name="root%d" % j)
-            nc.scalar.activation(root[:], sums[j][:].rearrange("p t n -> p n t"), ACT.Sqrt, bias=0.05)
-            roots.append(root)
-
-        def add_square(c, j):
-            if c == 0:
-                sums[j] = bank(sum_banks[j], [P, PACK, P], "sum%d" % j)
-            turn_and_add(sums[j], squares[c, j], c == 0, c == 2)
-
-        for c in range(3):
-            scale = gather_scales(c)
-            words = gather_words(c, 2, keep.tile([P, S], U32, name="picked_words%d" % c, align_bytes=64))
-            picked.append((words, scale))
-            pending = [square(c, j) for j in range(TILES)]
-            if c < 2:
-                for take_square in pending:
-                    take_square()
-            if c == 0:
-                add_square(0, 0)
-            if c == 1:
-                for step in ((0, 1), (1, 0), (1, 1), (0, 2)):
-                    add_square(*step)
-        for j in range(2):
-            pending[j]()
-            add_square(2, j)
-        for step in ((1, 2), (0, 3), (1, 3)):
-            add_square(*step)
-        for j in range(2):
-            root_of(j)
-        for j in range(2, TILES):
-            pending[j]()
-            add_square(2, j)
-        for j in range(2, TILES):
-            root_of(j)
-
-        e_scale = gather_scales(3)
-        w23_codes = keep.tile([P, 2 * N], U32, name="w23_codes", align_bytes=64)
-        w23 = quantize_pair(round_pair((w2_raw, w3_raw), "w23"), w23_codes, "w23")
-
-        w45_bf = keep.tile([P, 2, N, PACK], BF16, name="w45_bf", tag="w45_bf", align_bytes=64)
-        nc.vector.tensor_copy(w45_bf[:], w45_raw[:].rearrange("p a t c -> p a c t"))
-
-        nrm = keep.tile([P, TILES, P, PACK], BF16, name="nrm", tag="w23_bf", align_bytes=64)
-        nrm_codes = keep.tile([P, S], U32, name="nrm_codes", align_bytes=64)
-        nrm_scale = keep.tile([P, S], U8, name="nrm_scale", align_bytes=64)
-        halves = [slice(h * HALF, (h + 1) * HALF) for h in range(2)]
-
-        def apply_gain(j):
-            nc.vector.tensor_tensor(nrm[:, j], roots[j][:],
-                                    gain_t[:].unsqueeze(1).to_broadcast([P, P, PACK]), ALU.mult)
+                nc.scalar.activation(lengths[h][:, t, :], sums[t // 2][:, t % 2, :], ACT.Sqrt,
+                                     scale=gain_sq[:, t : t + 1], bias=gain_eps[:, t : t + 1])
 
         def quantize_nrm(h):
-            nc.vector.quantize_mx(out=nrm_codes[:, halves[h]].bitcast(FP8X4), scales=nrm_scale[:, halves[h]],
-                                  in_=nrm[:, 2 * h : 2 * h + 2].rearrange("p a n t -> p (a n t)"))
+            nc.vector.quantize_mx(out=nrm_mx[0][:, halves[h]].bitcast(FP8X4), scales=nrm_mx[1][:, halves[h]],
+                                  in_=nrm[h][:].rearrange("p n t -> p (n t)"))
 
-        apply_gain(0)
-        w45 = quantize_pair(w45_bf, keep.tile([P, 2 * N], U32, name="w45_codes", align_bytes=64), "w45")
-        apply_gain(1)
-        apply_gain(2)
-        quantize_nrm(0)
-        apply_gain(3)
-        e_picked = gather_words(3, 1, keep.tile([P, S], U32, name="picked_words3", align_bytes=64))
-        quantize_nrm(1)
+        ab_banks = ((2, 3, 0), (1, 6, 7))
 
-        gate = bank(1, [P, S], "gate")
-        nc.tensor.matmul_mx(out=gate[:], lhsT=w45[0][:, N : 2 * N].bitcast(FP8X4), lhsT_scale=w45[1][:, N : 2 * N],
-                            rhs=e_picked[:].bitcast(FP8X4), rhs_scale=e_scale[12:P, :], start=True, stop=False)
-        nc.tensor.matmul_mx(out=gate[:], lhsT=w45[0][:, 0:N].bitcast(FP8X4), lhsT_scale=w45[1][:, 0:N],
-                            rhs=nrm_codes[:].bitcast(FP8X4), rhs_scale=nrm_scale[:], start=False, stop=True)
-
-        ab_banks = ((0, 2, 7), (4, 3, 6))
-        dots = []
-        products = keep.tile([P, 2, 3, 2, N], F32, name="products")
-        for h in range(2):
-            for c in range(3):
-                words, scale = picked[c]
-                ab = bank(ab_banks[h][c], [P, 2, 2 * N], "ab%d%d" % (h, c))
+        def b_copies(h):
+            pairs = []
+            for c, picked in enumerate((x_mx, y_mx, z_mx)):
+                ab = bank(ab_banks[h][c], [P, 2, 2 * N], "ab%d%d" % (c, h))
                 for jj in range(2):
-                    tok = slice((2 * h + jj) * P, (2 * h + jj + 1) * P)
-                    nc.tensor.matmul_mx(
-                        out=ab[:, jj, :], lhsT=words[:, tok].bitcast(FP8X4), lhsT_scale=scale[4 * c : P, tok],
-                        rhs=w23[0][:].bitcast(FP8X4), rhs_scale=w23[1][:], start=True, stop=True)
-                b_half = keep.tile([P, 2, N], F32, name="b_half%d%d" % (h, c))
-                nc.scalar.activation(b_half[:], ab[:, :, N : 2 * N], ACT.Copy, scale=0.5)
-                nc.vector.tensor_tensor(products[:, h, c], ab[:, :, 0:N], b_half[:], ALU.mult)
-            dot = bank((5, 0)[h], [P, HALF], "dot%d" % h)
+                    product(ab[:, jj, :], picked, tiles[2 * h + jj], w23_mx, slice(0, 2 * N))
+                b_half = sbuf([P, 2, N], F32, "b_half%d%d" % (c, h))
+                if h == 0 and c == X:
+                    nc.vector.tensor_scalar(b_half[:], ab[:, :, N : 2 * N], 0.5, None, ALU.mult)
+                else:
+                    nc.scalar.activation(b_half[:], ab[:, :, N : 2 * N], ACT.Copy, scale=0.5)
+                pairs.append((ab, b_half))
+            return pairs
+
+        def dot_of(h, pairs):
+            products = sbuf([P, 3, 2, N], F32, "products%d" % h)
+            for c, (ab, b_half) in enumerate(pairs):
+                nc.vector.tensor_tensor(products[:, c], ab[:, :, 0:N], b_half[:], ALU.mult)
+            dot = bank(2 + h, [P, HALF], "dot%d" % h)
             for c in range(3):
                 for jj in range(2):
-                    nc.tensor.matmul(out=dot[:, jj * P : (jj + 1) * P], lhsT=products[:, h, c, jj, :], rhs=ident[:],
+                    nc.tensor.matmul(out=dot[:, tiles[jj]], lhsT=products[:, c, jj, :], rhs=ident[:],
                                      is_transpose=True, start=(c == 0 and jj == 0), stop=(c == 2 and jj == 1))
-            dots.append(dot)
+            return dot
 
-        sig = keep.tile([P, S], F32, name="sig")
-        for cols in halves:
-            nc.scalar.activation(sig[:, cols], gate[:, cols], ACT.Sigmoid)
-        gated = keep.tile([P, S], F32, name="gated")
-        res = keep.tile([P, S], F32, name="res")
-        for h, cols in enumerate(halves):
-            nc.vector.tensor_tensor(gated[:, cols], dots[h][:], sig[:, cols], ALU.mult)
-        for cols in halves:
+        w23_bf = sbuf([P, 2, N, PACK], BF16, "w23_bf")
+        w45_bf = sbuf([P, 2, N, PACK], BF16, "w45_bf")
+        for rounded, raw in ((w23_bf[:, 0], w23_raw[:, 0]), (w23_bf[:, 1], w23_raw[:, 1]), (w45_bf[:, 1], w5_raw[:])):
+            nc.gpsimd.tensor_scalar(rounded, raw.rearrange("p t c -> p c t"), 1.0, 0.0, ALU.mult, ALU.add)
+        w23_mx = quantize(w23_bf[:].rearrange("p a c t -> p (a c t)"), 2 * N, "w23")
+        nc.vector.tensor_tensor(w45_bf[:, 0].rearrange("p (c i) t -> p c t i", i=4),
+                                w4_raw[:].rearrange("p t (c i) -> p c t i", i=4),
+                                gain_sign[:].unsqueeze(1).unsqueeze(3).to_broadcast([P, N // 4, PACK, 4]), ALU.mult)
+        w45_mx = quantize(w45_bf[:].rearrange("p a c t -> p (a c t)"), 2 * N, "w45")
+
+        lengths_of(0)
+        lengths_of(1)
+        e_mx = (gather_words(E, 1), e_scale[4 * E : P])
+        nrm = [after_gather_of(E, 2048 * h, [P, HALF, PACK], BF16, "nrm%d" % h) for h in range(2)]
+        for h in range(2):
+            interleave(nc.vector.tensor_copy, nrm[h][:], lengths[h][:])
+        for h in range(2):
+            quantize_nrm(h)
+        pairs = [b_copies(h) for h in range(2)]
+
+        gates = [bank(4 + h, [P, HALF], "gate%d" % h) for h in range(2)]
+        w4_cols, w5_cols = slice(0, N), slice(N, 2 * N)
+        for h in range(2):
+            product(gates[h][:], w45_mx, w5_cols, e_mx, halves[h], start=True, stop=False)
+            product(gates[h][:], w45_mx, w4_cols, nrm_mx, halves[h], start=False, stop=True)
+        dots = [dot_of(h, pairs[h]) for h in range(2)]
+
+        sig = sbuf([P, S], F32, "sig")
+        gated = sbuf([P, S], F32, "gated")
+        res = sbuf([P, S], F32, "res")
+        pieces = ((0, slice(0, HALF)), (1, tiles[0]), (1, tiles[1]))
+        out_cols = (halves[0], tiles[2], tiles[3])
+        for (h, part), cols in zip(pieces, out_cols):
+            nc.scalar.activation(sig[:, cols], gates[h][:, part], ACT.Sigmoid)
+
+        def gate_piece(i):
+            h, part = pieces[i]
+            nc.vector.tensor_tensor(gated[:, out_cols[i]], dots[h][:, part], sig[:, out_cols[i]], ALU.mult)
+
+        def store_piece(i):
+            cols = out_cols[i]
             nc.vector.tensor_tensor(res[:, cols], gated[:, cols], skip_t[:, cols], ALU.add)
             nc.sync.dma_start(out[:, cols], res[:, cols])
+
+        gate_piece(0)
+        gate_piece(1)
+        store_piece(0)
+        gate_piece(2)
+        store_piece(1)
+        store_piece(2)

@@ -188,10 +188,7 @@ def tile_picked_ypainn_sigmoid_p_kernel(
                 for jj in range(2):
                     product(ab[:, jj, :], picked, tiles[2 * h + jj], w23_mx, slice(0, 2 * N))
                 b_half = sbuf([P, 2, N], F32, "b_half%d%d" % (c, h))
-                if h == 0 and c == X:
-                    nc.vector.tensor_scalar(b_half[:], ab[:, :, N : 2 * N], 0.5, None, ALU.mult)
-                else:
-                    nc.scalar.activation(b_half[:], ab[:, :, N : 2 * N], ACT.Copy, scale=0.5)
+                nc.scalar.activation(b_half[:], ab[:, :, N : 2 * N], ACT.Copy, scale=0.5)
                 pairs.append((ab, b_half))
             return pairs
 
@@ -208,13 +205,14 @@ def tile_picked_ypainn_sigmoid_p_kernel(
 
         w23_bf = sbuf([P, 2, N, PACK], BF16, "w23_bf")
         w45_bf = sbuf([P, 2, N, PACK], BF16, "w45_bf")
-        for rounded, raw in ((w23_bf[:, 0], w23_raw[:, 0]), (w23_bf[:, 1], w23_raw[:, 1]), (w45_bf[:, 1], w5_raw[:])):
-            nc.gpsimd.tensor_scalar(rounded, raw.rearrange("p t c -> p c t"), 1.0, 0.0, ALU.mult, ALU.add)
-        w23_mx = quantize(w23_bf[:].rearrange("p a c t -> p (a c t)"), 2 * N, "w23")
+        for i in range(2):
+            nc.gpsimd.tensor_scalar(w23_bf[:, i], w23_raw[:, i].rearrange("p t c -> p c t"), 1.0, 0.0, ALU.mult, ALU.add)
         nc.vector.tensor_tensor(w45_bf[:, 0].rearrange("p (c i) t -> p c t i", i=4),
                                 w4_raw[:].rearrange("p t (c i) -> p c t i", i=4),
                                 gain_sign[:].unsqueeze(1).unsqueeze(3).to_broadcast([P, N // 4, PACK, 4]), ALU.mult)
+        interleave(nc.vector.tensor_copy, w45_bf[:, 1], w5_raw[:])
         w45_mx = quantize(w45_bf[:].rearrange("p a c t -> p (a c t)"), 2 * N, "w45")
+        w23_mx = quantize(w23_bf[:].rearrange("p a c t -> p (a c t)"), 2 * N, "w23", "w45_bf")
 
         lengths_of(0)
         lengths_of(1)
@@ -251,8 +249,8 @@ def tile_picked_ypainn_sigmoid_p_kernel(
             nc.sync.dma_start(out[:, cols], res[:, cols])
 
         gate_piece(0)
-        gate_piece(1)
         store_piece(0)
-        gate_piece(2)
-        store_piece(1)
-        store_piece(2)
+        for i in (1, 2):
+            gate_piece(i)
+        for i in (1, 2):
+            store_piece(i)

@@ -47,10 +47,10 @@ def tile_picked_ypainn_sigmoid_p_kernel(
             return psum.tile(shape, F32, name=name, tag="bank%d" % b)
 
         offsets = keep.tile([P, S // 16], U16, name="offsets")
-        nc.sync.dma_start(offsets[:], offs)
 
         scale_win = [sbuf([P, T], U8, "scale_win%d" % c) for c in range(4)]
-        for c in (X, Z, Y, E):
+        nc.gpsimd.memset(scale_win[X][:].bitcast(I32), 0)
+        for c in (Z, Y, E):
             nc.vector.memset(scale_win[c][:].bitcast(I32), 0)
         shared = ctx.enter_context(tc.tile_pool(name="shared", bufs=1))
         word_win = [shared.tile([P, T], I32, name="word_win%d" % c, offset=c * WINDOW_BYTES, align_bytes=64) for c in range(4)]
@@ -84,6 +84,7 @@ def tile_picked_ypainn_sigmoid_p_kernel(
         skip_t = sbuf([P, S], F32, "skip_t")
 
         load_weight(w1_raw[:], w1)
+        nc.sync.dma_start(offsets[:], offs)
         load_scales(X, nc.sync)
         load_words(X)
         nc.sync.dma_start(gain_t[:], gain.rearrange("(p j) o -> p (j o)", j=PACK))
@@ -204,15 +205,17 @@ def tile_picked_ypainn_sigmoid_p_kernel(
             return dot
 
         w23_bf = sbuf([P, 2, N, PACK], BF16, "w23_bf")
-        w45_bf = sbuf([P, 2, N, PACK], BF16, "w45_bf")
+        w4_bf = sbuf([P, N, PACK], BF16, "w4_bf")
+        w5_bf = sbuf([P, N, PACK], BF16, "w5_bf")
         for i in range(2):
             nc.gpsimd.tensor_scalar(w23_bf[:, i], w23_raw[:, i].rearrange("p t c -> p c t"), 1.0, 0.0, ALU.mult, ALU.add)
-        nc.vector.tensor_tensor(w45_bf[:, 0].rearrange("p (c i) t -> p c t i", i=4),
+        nc.vector.tensor_tensor(w4_bf[:].rearrange("p (c i) t -> p c t i", i=4),
                                 w4_raw[:].rearrange("p t (c i) -> p c t i", i=4),
                                 gain_sign[:].unsqueeze(1).unsqueeze(3).to_broadcast([P, N // 4, PACK, 4]), ALU.mult)
-        interleave(nc.vector.tensor_copy, w45_bf[:, 1], w5_raw[:])
-        w45_mx = quantize(w45_bf[:].rearrange("p a c t -> p (a c t)"), 2 * N, "w45")
-        w23_mx = quantize(w23_bf[:].rearrange("p a c t -> p (a c t)"), 2 * N, "w23", "w45_bf")
+        interleave(nc.vector.tensor_copy, w5_bf[:], w5_raw[:])
+        w4_mx = quantize(w4_bf[:].rearrange("p c t -> p (c t)"), N, "w4")
+        w5_mx = quantize(w5_bf[:].rearrange("p c t -> p (c t)"), N, "w5")
+        w23_mx = quantize(w23_bf[:].rearrange("p a c t -> p (a c t)"), 2 * N, "w23", "w4_bf")
 
         lengths_of(0)
         lengths_of(1)
@@ -225,10 +228,9 @@ def tile_picked_ypainn_sigmoid_p_kernel(
         pairs = [b_copies(h) for h in range(2)]
 
         gates = [bank(4 + h, [P, HALF], "gate%d" % h) for h in range(2)]
-        w4_cols, w5_cols = slice(0, N), slice(N, 2 * N)
         for h in range(2):
-            product(gates[h][:], w45_mx, w5_cols, e_mx, halves[h], start=True, stop=False)
-            product(gates[h][:], w45_mx, w4_cols, nrm_mx, halves[h], start=False, stop=True)
+            product(gates[h][:], w5_mx, slice(0, N), e_mx, halves[h], start=True, stop=False)
+            product(gates[h][:], w4_mx, slice(0, N), nrm_mx, halves[h], start=False, stop=True)
         dots = [dot_of(h, pairs[h]) for h in range(2)]
 
         sig = sbuf([P, S], F32, "sig")

@@ -23,7 +23,6 @@ EPS = 0.05
 W1_SCALAR_SHARE = 320
 FLOPS = 2 * K * S * (3 * H + 7 * N) + 2 * H * S * N
 X, Y, Z, E = range(4)
-WINDOW_BYTES = 4 * T
 
 
 def tile_picked_ypainn_sigmoid_p_kernel(
@@ -52,11 +51,7 @@ def tile_picked_ypainn_sigmoid_p_kernel(
         nc.gpsimd.memset(scale_win[X][:].bitcast(I32), 0)
         for c in (Z, Y, E):
             nc.vector.memset(scale_win[c][:].bitcast(I32), 0)
-        shared = ctx.enter_context(tc.tile_pool(name="shared", bufs=1))
-        word_win = [shared.tile([P, T], I32, name="word_win%d" % c, offset=c * WINDOW_BYTES, align_bytes=64) for c in range(4)]
-
-        def after_gather_of(c, at, shape, dtype, name):
-            return shared.tile(shape, dtype, name=name, offset=c * WINDOW_BYTES + at, align_bytes=64)
+        word_win = [sbuf([P, T], I32, "word_win%d" % c) for c in range(4)]
 
         one = sbuf([P, 1], F32, "one")
         nc.gpsimd.memset(one[:], 1.0)
@@ -73,8 +68,8 @@ def tile_picked_ypainn_sigmoid_p_kernel(
         def load_words(c):
             nc.sync.dma_start(word_win[c][:], words_in[c][0].rearrange("p n t -> p (n t)").bitcast(I32))
 
-        def load_weight(raw, w):
-            nc.sync.dma_start(raw, w.rearrange("(p j) c -> p j c", j=PACK))
+        def by_slot(w):
+            return w.rearrange("(p j) c -> p j c", j=PACK)
 
         w1_raw = sbuf([P, PACK, H], F32, "w1_raw")
         w23_raw = sbuf([P, 2, PACK, N], F32, "w23_raw")
@@ -83,7 +78,7 @@ def tile_picked_ypainn_sigmoid_p_kernel(
         gain_t = sbuf([P, PACK], F32, "gain_t")
         skip_t = sbuf([P, S], F32, "skip_t")
 
-        load_weight(w1_raw[:], w1)
+        nc.sync.dma_start(w1_raw[:], by_slot(w1))
         nc.sync.dma_start(offsets[:], offs)
         load_scales(X, nc.sync)
         load_words(X)
@@ -91,10 +86,10 @@ def tile_picked_ypainn_sigmoid_p_kernel(
         load_scales(Y, nc.sync)
         load_words(Y)
         load_words(Z)
-        load_weight(w23_raw[:, 0], w2)
-        load_weight(w23_raw[:, 1], w3)
-        load_weight(w4_raw[:], w4)
-        load_weight(w5_raw[:], w5)
+        nc.sync.dma_start(w23_raw[:, 0], by_slot(w2))
+        nc.sync.dma_start(w23_raw[:, 1], by_slot(w3))
+        nc.sync.dma_start(w4_raw[:], by_slot(w4))
+        nc.sync.dma_start(w5_raw[:], by_slot(w5))
         load_words(E)
         nc.sync.dma_start(skip_t[:], skip)
         load_scales(Z, nc.gpsimd)
@@ -103,9 +98,8 @@ def tile_picked_ypainn_sigmoid_p_kernel(
         def interleave(copy, grouped, planes):
             copy(grouped.rearrange("p (c i) t -> p c t i", i=4), planes.rearrange("p t (c i) -> p c t i", i=4))
 
-        w1_bf = sbuf([P, H, PACK], BF16, "w1_bf")
-        interleave(nc.scalar.copy, w1_bf[:, :W1_SCALAR_SHARE, :], w1_raw[:, :, :W1_SCALAR_SHARE])
-        interleave(nc.vector.tensor_copy, w1_bf[:, W1_SCALAR_SHARE:, :], w1_raw[:, :, W1_SCALAR_SHARE:])
+        def interleave_on_gpsimd(grouped, planes):
+            nc.gpsimd.tensor_scalar(grouped, planes.rearrange("p t c -> p c t"), 1.0, 0.0, ALU.mult, ALU.add)
 
         def quantize(values, width, name, tag=None):
             codes = sbuf([P, width], U32, name + "_codes", tag)
@@ -113,16 +107,15 @@ def tile_picked_ypainn_sigmoid_p_kernel(
             nc.vector.quantize_mx(out=codes[:].bitcast(FP8X4), scales=scale[:], in_=values)
             return codes, scale
 
-        def gather_scales(c, scale):
+        def gather_scales(c, tag=None):
+            scale = sbuf([P, S], U8, "picked_scale%d" % c, tag)
             nc.vector.tensor_copy(scale[:], scale_win[c][:].indirect(offsets[:]))
-            return scale
+            return scale[4 * c : P]
 
-        def gather_words(c, pieces):
+        def gather_words(c, cuts):
             words = sbuf([P, S], U32, "picked_words%d" % c)
-            width = S // pieces
-            for h in range(pieces):
-                nc.vector.tensor_copy(words[:, h * width : (h + 1) * width],
-                                      word_win[c][:].bitcast(U32).indirect(offsets[:, h * width // 16 : (h + 1) * width // 16]))
+            for lo, hi in zip(cuts, cuts[1:]):
+                nc.vector.tensor_copy(words[:, lo:hi], word_win[c][:].bitcast(U32).indirect(offsets[:, lo // 16 : hi // 16]))
             return words
 
         def product(result, lhs, lhs_cols, rhs, rhs_cols, start=True, stop=True):
@@ -130,7 +123,10 @@ def tile_picked_ypainn_sigmoid_p_kernel(
                                 rhs=rhs[0][:, rhs_cols].bitcast(FP8X4), rhs_scale=rhs[1][:, rhs_cols],
                                 start=start, stop=stop)
 
-        x_scale = gather_scales(X, sbuf([P, S], U8, "picked_scale_x"))
+        x_scale = gather_scales(X)
+        w1_bf = sbuf([P, H, PACK], BF16, "w1_bf")
+        interleave(nc.scalar.copy, w1_bf[:, :W1_SCALAR_SHARE, :], w1_raw[:, :, :W1_SCALAR_SHARE])
+        interleave(nc.vector.tensor_copy, w1_bf[:, W1_SCALAR_SHARE:, :], w1_raw[:, :, W1_SCALAR_SHARE:])
         w1_mx = quantize(w1_bf[:].rearrange("p c t -> p (c t)"), H, "w1", "scale_win%d" % X)
 
         gain_sq = sbuf([P, PACK], F32, "gain_sq")
@@ -150,21 +146,19 @@ def tile_picked_ypainn_sigmoid_p_kernel(
                 squares.append(sq)
             return squares
 
-        x_mx = (gather_words(X, 2), x_scale[4 * X : P])
+        x_mx = (gather_words(X, (0, HALF, S)), x_scale)
         x_squares = squares_of(X, x_mx, (0, 1, 2, 3))
-        y_scale = gather_scales(Y, sbuf([P, S], U8, "picked_scale_y"))
-        y_mx = (gather_words(Y, 2), y_scale[4 * Y : P])
+        y_scale = gather_scales(Y)
+        y_mx = (gather_words(Y, (0, HALF, S)), y_scale)
         y_squares = squares_of(Y, y_mx, (4, 5, 0, 1))
-        z_scale = gather_scales(Z, after_gather_of(Y, 0, [P, S], U8, "picked_scale_z"))
-        z_mx = (gather_words(Z, 2), z_scale[4 * Z : P])
-        e_scale = gather_scales(E, after_gather_of(Z, 0, [P, S], U8, "picked_scale_e"))
+        z_scale = gather_scales(Z, "word_win%d" % Y)
+        z_mx = (gather_words(Z, (0, P, HALF, S)), z_scale)
         z_squares = squares_of(Z, z_mx, (2, 3, 0, 1))
 
         sum_banks = ((6, 7), (4, 5))
         lengths = [sbuf([P, PACK, HALF], BF16, "lengths%d" % h) for h in range(2)]
-        nrm_mx = (sbuf([P, S], U32, "nrm_codes"), sbuf([P, S], U8, "nrm_scale"))
 
-        def lengths_of(h):
+        def sums_of(h):
             sums = [bank(sum_banks[h][u], [P, 2, HALF], "sum%d%d" % (h, u)) for u in range(2)]
             for c, squares in enumerate((x_squares, y_squares, z_squares)):
                 for jj in range(2):
@@ -176,70 +170,67 @@ def tile_picked_ypainn_sigmoid_p_kernel(
                 nc.scalar.activation(lengths[h][:, t, :], sums[t // 2][:, t % 2, :], ACT.Sqrt,
                                      scale=gain_sq[:, t : t + 1], bias=gain_eps[:, t : t + 1])
 
-        def quantize_nrm(h):
-            nc.vector.quantize_mx(out=nrm_mx[0][:, halves[h]].bitcast(FP8X4), scales=nrm_mx[1][:, halves[h]],
-                                  in_=nrm[h][:].rearrange("p n t -> p (n t)"))
-
-        ab_banks = ((2, 3, 0), (1, 6, 7))
-
-        def b_copies(h):
-            pairs = []
-            for c, picked in enumerate((x_mx, y_mx, z_mx)):
-                ab = bank(ab_banks[h][c], [P, 2, 2 * N], "ab%d%d" % (c, h))
-                for jj in range(2):
-                    product(ab[:, jj, :], picked, tiles[2 * h + jj], w23_mx, slice(0, 2 * N))
-                b_half = sbuf([P, 2, N], F32, "b_half%d%d" % (c, h))
-                nc.scalar.activation(b_half[:], ab[:, :, N : 2 * N], ACT.Copy, scale=0.5)
-                pairs.append((ab, b_half))
-            return pairs
-
-        def dot_of(h, pairs):
-            products = sbuf([P, 3, 2, N], F32, "products%d" % h)
-            for c, (ab, b_half) in enumerate(pairs):
-                nc.vector.tensor_tensor(products[:, c], ab[:, :, 0:N], b_half[:], ALU.mult)
-            dot = bank(2 + h, [P, HALF], "dot%d" % h)
-            for c in range(3):
-                for jj in range(2):
-                    nc.tensor.matmul(out=dot[:, tiles[jj]], lhsT=products[:, c, jj, :], rhs=ident[:],
-                                     is_transpose=True, start=(c == 0 and jj == 0), stop=(c == 2 and jj == 1))
-            return dot
+        sums_of(0)
+        sums_of(1)
+        e_scale = gather_scales(E, "word_win%d" % Z)
 
         w23_bf = sbuf([P, 2, N, PACK], BF16, "w23_bf")
-        w4_bf = sbuf([P, N, PACK], BF16, "w4_bf")
-        w5_bf = sbuf([P, N, PACK], BF16, "w5_bf")
+        w45_bf = sbuf([P, 2, N, PACK], BF16, "w45_bf")
         for i in range(2):
-            nc.gpsimd.tensor_scalar(w23_bf[:, i], w23_raw[:, i].rearrange("p t c -> p c t"), 1.0, 0.0, ALU.mult, ALU.add)
-        nc.vector.tensor_tensor(w4_bf[:].rearrange("p (c i) t -> p c t i", i=4),
+            interleave_on_gpsimd(w23_bf[:, i], w23_raw[:, i])
+        interleave_on_gpsimd(w45_bf[:, 1], w5_raw[:])
+        nc.vector.tensor_tensor(w45_bf[:, 0].rearrange("p (c i) t -> p c t i", i=4),
                                 w4_raw[:].rearrange("p t (c i) -> p c t i", i=4),
                                 gain_sign[:].unsqueeze(1).unsqueeze(3).to_broadcast([P, N // 4, PACK, 4]), ALU.mult)
-        interleave(nc.vector.tensor_copy, w5_bf[:], w5_raw[:])
-        w4_mx = quantize(w4_bf[:].rearrange("p c t -> p (c t)"), N, "w4")
-        w5_mx = quantize(w5_bf[:].rearrange("p c t -> p (c t)"), N, "w5")
-        w23_mx = quantize(w23_bf[:].rearrange("p a c t -> p (a c t)"), 2 * N, "w23", "w4_bf")
+        w23_mx = quantize(w23_bf[:].rearrange("p a c t -> p (a c t)"), 2 * N, "w23")
+        w45_mx = quantize(w45_bf[:].rearrange("p a c t -> p (a c t)"), 2 * N, "w45")
 
-        lengths_of(0)
-        lengths_of(1)
-        e_mx = (gather_words(E, 1), e_scale[4 * E : P])
-        nrm = [after_gather_of(E, 2048 * h, [P, HALF, PACK], BF16, "nrm%d" % h) for h in range(2)]
-        for h in range(2):
-            interleave(nc.vector.tensor_copy, nrm[h][:], lengths[h][:])
-        for h in range(2):
-            quantize_nrm(h)
-        pairs = [b_copies(h) for h in range(2)]
+        ab_banks = ((2, 3, 0), (1, 6, 7))
+        products = [sbuf([P, 3, 2, N], F32, "products%d" % h) for h in range(2)]
 
-        gates = [bank(4 + h, [P, HALF], "gate%d" % h) for h in range(2)]
+        def ab_of(h, c):
+            ab = bank(ab_banks[h][c], [P, 2, 2 * N], "ab%d%d" % (c, h))
+            for jj in range(2):
+                product(ab[:, jj, :], (x_mx, y_mx, z_mx)[c], tiles[2 * h + jj], w23_mx, slice(0, 2 * N))
+            return ab, sbuf([P, 2, N], F32, "b_half%d%d" % (c, h))
+
+        def multiply(h, c, pair):
+            nc.vector.tensor_tensor(products[h][:, c], pair[0][:, :, 0:N], pair[1][:], ALU.mult)
+
+        e_mx = (gather_words(E, (0, S)), e_scale)
+        pairs = {(0, X): ab_of(0, X)}
+        on_scalar = ((0, Y), (0, Z), (1, X), (1, Y), (1, Z))
+        nc.vector.tensor_scalar(pairs[0, X][1][:], pairs[0, X][0][:, :, N : 2 * N], 0.5, None, ALU.mult)
+        for key in on_scalar:
+            pairs[key] = ab_of(*key)
+            nc.scalar.activation(pairs[key][1][:], pairs[key][0][:, :, N : 2 * N], ACT.Copy, scale=0.5)
+        nrm = sbuf([P, S, PACK], BF16, "nrm")
+        interleave_on_gpsimd(nrm[:, halves[0], :], lengths[0][:])
+        interleave(nc.vector.tensor_copy, nrm[:, halves[1], :], lengths[1][:])
+        for key in ((0, X), (0, Y)):
+            multiply(*key, pairs[key])
+        nrm_mx = quantize(nrm[:].rearrange("p n t -> p (n t)"), S, "nrm")
+        for key in on_scalar[1:]:
+            multiply(*key, pairs[key])
+
+        gate = bank(4, [P, S], "gate")
+        product(gate[:], w45_mx, slice(N, 2 * N), e_mx, slice(0, S), start=True, stop=False)
+        product(gate[:], w45_mx, slice(0, N), nrm_mx, slice(0, S), start=False, stop=True)
+
+        dots = [bank(2 + h, [P, HALF], "dot%d" % h) for h in range(2)]
         for h in range(2):
-            product(gates[h][:], w5_mx, slice(0, N), e_mx, halves[h], start=True, stop=False)
-            product(gates[h][:], w4_mx, slice(0, N), nrm_mx, halves[h], start=False, stop=True)
-        dots = [dot_of(h, pairs[h]) for h in range(2)]
+            for c in range(3):
+                for jj in range(2):
+                    nc.tensor.matmul(out=dots[h][:, tiles[jj]], lhsT=products[h][:, c, jj, :], rhs=ident[:],
+                                     is_transpose=True, start=(c == 0 and jj == 0), stop=(c == 2 and jj == 1))
 
         sig = sbuf([P, S], F32, "sig")
         gated = sbuf([P, S], F32, "gated")
         res = sbuf([P, S], F32, "res")
         pieces = ((0, slice(0, HALF)), (1, tiles[0]), (1, tiles[1]))
         out_cols = (halves[0], tiles[2], tiles[3])
-        for (h, part), cols in zip(pieces, out_cols):
-            nc.scalar.activation(sig[:, cols], gates[h][:, part], ACT.Sigmoid)
+        for cols in out_cols:
+            nc.scalar.activation(sig[:, cols], gate[:, cols], ACT.Sigmoid)
 
         def gate_piece(i):
             h, part = pieces[i]
@@ -251,8 +242,8 @@ def tile_picked_ypainn_sigmoid_p_kernel(
             nc.sync.dma_start(out[:, cols], res[:, cols])
 
         gate_piece(0)
+        gate_piece(1)
         store_piece(0)
-        for i in (1, 2):
-            gate_piece(i)
-        for i in (1, 2):
-            store_piece(i)
+        gate_piece(2)
+        store_piece(1)
+        store_piece(2)

@@ -98,9 +98,6 @@ def tile_picked_ypainn_sigmoid_p_kernel(
         def interleave(copy, grouped, planes):
             copy(grouped.rearrange("p (c i) t -> p c t i", i=4), planes.rearrange("p t (c i) -> p c t i", i=4))
 
-        def interleave_on_gpsimd(grouped, planes):
-            nc.gpsimd.tensor_scalar(grouped, planes.rearrange("p t c -> p c t"), 1.0, 0.0, ALU.mult, ALU.add)
-
         def quantize(values, width, name, tag=None):
             codes = sbuf([P, width], U32, name + "_codes", tag)
             scale = sbuf([P, width], U8, name + "_scale")
@@ -176,13 +173,13 @@ def tile_picked_ypainn_sigmoid_p_kernel(
 
         w23_bf = sbuf([P, 2, N, PACK], BF16, "w23_bf")
         w45_bf = sbuf([P, 2, N, PACK], BF16, "w45_bf")
-        for i in range(2):
-            interleave_on_gpsimd(w23_bf[:, i], w23_raw[:, i])
-        interleave_on_gpsimd(w45_bf[:, 1], w5_raw[:])
+        nc.vector.tensor_copy(w23_bf[:].rearrange("p a (c i) t -> p a c t i", i=4),
+                              w23_raw[:].rearrange("p a t (c i) -> p a c t i", i=4))
         nc.vector.tensor_tensor(w45_bf[:, 0].rearrange("p (c i) t -> p c t i", i=4),
                                 w4_raw[:].rearrange("p t (c i) -> p c t i", i=4),
                                 gain_sign[:].unsqueeze(1).unsqueeze(3).to_broadcast([P, N // 4, PACK, 4]), ALU.mult)
         w23_mx = quantize(w23_bf[:].rearrange("p a c t -> p (a c t)"), 2 * N, "w23")
+        interleave(nc.vector.tensor_copy, w45_bf[:, 1], w5_raw[:])
         w45_mx = quantize(w45_bf[:].rearrange("p a c t -> p (a c t)"), 2 * N, "w45")
 
         ab_banks = ((2, 3, 0), (1, 6, 7))
@@ -198,19 +195,17 @@ def tile_picked_ypainn_sigmoid_p_kernel(
             nc.vector.tensor_tensor(products[h][:, c], pair[0][:, :, 0:N], pair[1][:], ALU.mult)
 
         e_mx = (gather_words(E, (0, S)), e_scale)
-        pairs = {(0, X): ab_of(0, X)}
-        on_scalar = ((0, Y), (0, Z), (1, X), (1, Y), (1, Z))
-        nc.vector.tensor_scalar(pairs[0, X][1][:], pairs[0, X][0][:, :, N : 2 * N], 0.5, None, ALU.mult)
-        for key in on_scalar:
+        pairs = {}
+        keys = [(h, c) for h in range(2) for c in (X, Y, Z)]
+        for key in keys:
             pairs[key] = ab_of(*key)
             nc.scalar.activation(pairs[key][1][:], pairs[key][0][:, :, N : 2 * N], ACT.Copy, scale=0.5)
         nrm = sbuf([P, S, PACK], BF16, "nrm")
-        interleave_on_gpsimd(nrm[:, halves[0], :], lengths[0][:])
-        interleave(nc.vector.tensor_copy, nrm[:, halves[1], :], lengths[1][:])
-        for key in ((0, X), (0, Y)):
-            multiply(*key, pairs[key])
+        for h in range(2):
+            interleave(nc.vector.tensor_copy, nrm[:, halves[h], :], lengths[h][:])
+        multiply(*keys[0], pairs[keys[0]])
         nrm_mx = quantize(nrm[:].rearrange("p n t -> p (n t)"), S, "nrm")
-        for key in on_scalar[1:]:
+        for key in keys[1:]:
             multiply(*key, pairs[key])
 
         gate = bank(4, [P, S], "gate")

@@ -172,15 +172,17 @@ def tile_picked_ypainn_sigmoid_p_kernel(
         e_scale = gather_scales(E, "word_win%d" % Z)
 
         w23_bf = sbuf([P, 2, N, PACK], BF16, "w23_bf")
-        w45_bf = sbuf([P, 2, N, PACK], BF16, "w45_bf")
-        nc.vector.tensor_copy(w23_bf[:].rearrange("p a (c i) t -> p a c t i", i=4),
-                              w23_raw[:].rearrange("p a t (c i) -> p a c t i", i=4))
-        nc.vector.tensor_tensor(w45_bf[:, 0].rearrange("p (c i) t -> p c t i", i=4),
+        w4_bf = sbuf([P, N, PACK], BF16, "w4_bf")
+        w5_bf = sbuf([P, N, PACK], BF16, "w5_bf")
+        for i in range(2):
+            nc.gpsimd.tensor_scalar(w23_bf[:, i], w23_raw[:, i].rearrange("p t c -> p c t"), 1.0, 0.0, ALU.mult, ALU.add)
+        nc.vector.tensor_tensor(w4_bf[:].rearrange("p (c i) t -> p c t i", i=4),
                                 w4_raw[:].rearrange("p t (c i) -> p c t i", i=4),
                                 gain_sign[:].unsqueeze(1).unsqueeze(3).to_broadcast([P, N // 4, PACK, 4]), ALU.mult)
         w23_mx = quantize(w23_bf[:].rearrange("p a c t -> p (a c t)"), 2 * N, "w23")
-        interleave(nc.vector.tensor_copy, w45_bf[:, 1], w5_raw[:])
-        w45_mx = quantize(w45_bf[:].rearrange("p a c t -> p (a c t)"), 2 * N, "w45")
+        interleave(nc.vector.tensor_copy, w5_bf[:], w5_raw[:])
+        w4_mx = quantize(w4_bf[:].rearrange("p c t -> p (c t)"), N, "w4")
+        w5_mx = quantize(w5_bf[:].rearrange("p c t -> p (c t)"), N, "w5")
 
         ab_banks = ((2, 3, 0), (1, 6, 7))
         products = [sbuf([P, 3, 2, N], F32, "products%d" % h) for h in range(2)]
@@ -209,8 +211,8 @@ def tile_picked_ypainn_sigmoid_p_kernel(
             multiply(*key, pairs[key])
 
         gate = bank(4, [P, S], "gate")
-        product(gate[:], w45_mx, slice(N, 2 * N), e_mx, slice(0, S), start=True, stop=False)
-        product(gate[:], w45_mx, slice(0, N), nrm_mx, slice(0, S), start=False, stop=True)
+        product(gate[:], w5_mx, slice(0, N), e_mx, slice(0, S), start=True, stop=False)
+        product(gate[:], w4_mx, slice(0, N), nrm_mx, slice(0, S), start=False, stop=True)
 
         dots = [bank(2 + h, [P, HALF], "dot%d" % h) for h in range(2)]
         for h in range(2):

@@ -20,7 +20,7 @@ K, T, S, H, N = 512, 2048, 512, 512, 128
 HALF = S // 2
 TILES = S // P
 EPS = 0.05
-W1_SCALAR_SHARE = 320
+W1_SCALAR_SHARE = 256
 FLOPS = 2 * K * S * (3 * H + 7 * N) + 2 * H * S * N
 X, Y, Z, E = range(4)
 
@@ -78,9 +78,10 @@ def tile_picked_ypainn_sigmoid_p_kernel(
         gain_t = sbuf([P, PACK], F32, "gain_t")
         skip_t = sbuf([P, S], F32, "skip_t")
 
-        nc.sync.dma_start(w1_raw[:], by_slot(w1))
+        nc.sync.dma_start(w1_raw[:, :2, :], by_slot(w1)[:, :2, :])
         nc.sync.dma_start(offsets[:], offs)
         load_scales(X, nc.sync)
+        nc.sync.dma_start(w1_raw[:, 2:, :], by_slot(w1)[:, 2:, :])
         load_words(X)
         nc.sync.dma_start(gain_t[:], gain.rearrange("(p j) o -> p (j o)", j=PACK))
         load_scales(Y, nc.sync)
@@ -98,8 +99,8 @@ def tile_picked_ypainn_sigmoid_p_kernel(
         def interleave(copy, grouped, planes):
             copy(grouped.rearrange("p (c i) t -> p c t i", i=4), planes.rearrange("p t (c i) -> p c t i", i=4))
 
-        def quantize(values, width, name, tag=None):
-            codes = sbuf([P, width], U32, name + "_codes", tag)
+        def quantize(values, width, name):
+            codes = sbuf([P, width], U32, name + "_codes")
             scale = sbuf([P, width], U8, name + "_scale")
             nc.vector.quantize_mx(out=codes[:].bitcast(FP8X4), scales=scale[:], in_=values)
             return codes, scale
@@ -124,7 +125,7 @@ def tile_picked_ypainn_sigmoid_p_kernel(
         w1_bf = sbuf([P, H, PACK], BF16, "w1_bf")
         interleave(nc.scalar.copy, w1_bf[:, :W1_SCALAR_SHARE, :], w1_raw[:, :, :W1_SCALAR_SHARE])
         interleave(nc.vector.tensor_copy, w1_bf[:, W1_SCALAR_SHARE:, :], w1_raw[:, :, W1_SCALAR_SHARE:])
-        w1_mx = quantize(w1_bf[:].rearrange("p c t -> p (c t)"), H, "w1", "scale_win%d" % X)
+        w1_mx = quantize(w1_bf[:].rearrange("p c t -> p (c t)"), H, "w1")
 
         gain_sq = sbuf([P, PACK], F32, "gain_sq")
         gain_eps = sbuf([P, PACK], F32, "gain_eps")
@@ -146,29 +147,30 @@ def tile_picked_ypainn_sigmoid_p_kernel(
         x_mx = (gather_words(X, (0, HALF, S)), x_scale)
         x_squares = squares_of(X, x_mx, (0, 1, 2, 3))
         y_scale = gather_scales(Y)
-        y_mx = (gather_words(Y, (0, HALF, S)), y_scale)
+        y_mx = (gather_words(Y, (0, P, HALF, S)), y_scale)
         y_squares = squares_of(Y, y_mx, (4, 5, 0, 1))
         z_scale = gather_scales(Z, "word_win%d" % Y)
         z_mx = (gather_words(Z, (0, P, HALF, S)), z_scale)
-        z_squares = squares_of(Z, z_mx, (2, 3, 0, 1))
+        z_squares = squares_of(Z, z_mx, (2, 3, 4, 5))
 
-        sum_banks = ((6, 7), (4, 5))
+        sum_banks = ((6, 7), (2, 1))
         lengths = [sbuf([P, PACK, HALF], BF16, "lengths%d" % h) for h in range(2)]
 
-        def sums_of(h):
+        squares = (x_squares, y_squares, z_squares)
+
+        def sums_of(h, terms):
             sums = [bank(sum_banks[h][u], [P, 2, HALF], "sum%d%d" % (h, u)) for u in range(2)]
-            for c, squares in enumerate((x_squares, y_squares, z_squares)):
-                for jj in range(2):
-                    for t in range(PACK):
-                        nc.tensor.matmul(out=sums[t // 2][:, t % 2, tiles[jj]], lhsT=squares[2 * h + jj][:, t, :],
-                                         rhs=ident[:], is_transpose=True,
-                                         start=(c == X and jj == 0 and t % 2 == 0), stop=(c == Z and jj == 1 and t % 2 == 1))
+            for c, jj in terms:
+                for t in range(PACK):
+                    nc.tensor.matmul(out=sums[t // 2][:, t % 2, tiles[jj]], lhsT=squares[c][2 * h + jj][:, t, :],
+                                     rhs=ident[:], is_transpose=True,
+                                     start=((c, jj) == terms[0] and t % 2 == 0), stop=((c, jj) == terms[-1] and t % 2 == 1))
             for t in range(PACK):
                 nc.scalar.activation(lengths[h][:, t, :], sums[t // 2][:, t % 2, :], ACT.Sqrt,
                                      scale=gain_sq[:, t : t + 1], bias=gain_eps[:, t : t + 1])
 
-        sums_of(0)
-        sums_of(1)
+        sums_of(0, [(Y, 0), (X, 0), (X, 1), (Y, 1), (Z, 0), (Z, 1)])
+        sums_of(1, [(c, jj) for c in (X, Y, Z) for jj in range(2)])
         e_scale = gather_scales(E, "word_win%d" % Z)
 
         w23_bf = sbuf([P, 2, N, PACK], BF16, "w23_bf")
@@ -184,7 +186,7 @@ def tile_picked_ypainn_sigmoid_p_kernel(
         w4_mx = quantize(w4_bf[:].rearrange("p c t -> p (c t)"), N, "w4")
         w5_mx = quantize(w5_bf[:].rearrange("p c t -> p (c t)"), N, "w5")
 
-        ab_banks = ((2, 3, 0), (1, 6, 7))
+        ab_banks = ((0, 3, 4), (5, 6, 7))
         products = [sbuf([P, 3, 2, N], F32, "products%d" % h) for h in range(2)]
 
         def ab_of(h, c):
@@ -210,11 +212,11 @@ def tile_picked_ypainn_sigmoid_p_kernel(
         for key in keys[1:]:
             multiply(*key, pairs[key])
 
-        gate = bank(4, [P, S], "gate")
+        gate = bank(2, [P, S], "gate")
         product(gate[:], w5_mx, slice(0, N), e_mx, slice(0, S), start=True, stop=False)
         product(gate[:], w4_mx, slice(0, N), nrm_mx, slice(0, S), start=False, stop=True)
 
-        dots = [bank(2 + h, [P, HALF], "dot%d" % h) for h in range(2)]
+        dots = [bank(3 * h, [P, HALF], "dot%d" % h) for h in range(2)]
         for h in range(2):
             for c in range(3):
                 for jj in range(2):

@@ -20,7 +20,7 @@ K, T, S, H, N = 512, 2048, 512, 512, 128
 HALF = S // 2
 TILES = S // P
 EPS = 0.05
-W1_SCALAR_SHARE = 256
+W1_SCALAR_SHARE = 320
 FLOPS = 2 * K * S * (3 * H + 7 * N) + 2 * H * S * N
 X, Y, Z, E = range(4)
 
@@ -78,10 +78,9 @@ def tile_picked_ypainn_sigmoid_p_kernel(
         gain_t = sbuf([P, PACK], F32, "gain_t")
         skip_t = sbuf([P, S], F32, "skip_t")
 
-        nc.sync.dma_start(w1_raw[:, :2, :], by_slot(w1)[:, :2, :])
+        nc.sync.dma_start(w1_raw[:], by_slot(w1))
         nc.sync.dma_start(offsets[:], offs)
         load_scales(X, nc.sync)
-        nc.sync.dma_start(w1_raw[:, 2:, :], by_slot(w1)[:, 2:, :])
         load_words(X)
         nc.sync.dma_start(gain_t[:], gain.rearrange("(p j) o -> p (j o)", j=PACK))
         load_scales(Y, nc.sync)
@@ -99,8 +98,8 @@ def tile_picked_ypainn_sigmoid_p_kernel(
         def interleave(copy, grouped, planes):
             copy(grouped.rearrange("p (c i) t -> p c t i", i=4), planes.rearrange("p t (c i) -> p c t i", i=4))
 
-        def quantize(values, width, name):
-            codes = sbuf([P, width], U32, name + "_codes")
+        def quantize(values, width, name, tag=None):
+            codes = sbuf([P, width], U32, name + "_codes", tag)
             scale = sbuf([P, width], U8, name + "_scale")
             nc.vector.quantize_mx(out=codes[:].bitcast(FP8X4), scales=scale[:], in_=values)
             return codes, scale
@@ -125,7 +124,7 @@ def tile_picked_ypainn_sigmoid_p_kernel(
         w1_bf = sbuf([P, H, PACK], BF16, "w1_bf")
         interleave(nc.scalar.copy, w1_bf[:, :W1_SCALAR_SHARE, :], w1_raw[:, :, :W1_SCALAR_SHARE])
         interleave(nc.vector.tensor_copy, w1_bf[:, W1_SCALAR_SHARE:, :], w1_raw[:, :, W1_SCALAR_SHARE:])
-        w1_mx = quantize(w1_bf[:].rearrange("p c t -> p (c t)"), H, "w1")
+        w1_mx = quantize(w1_bf[:].rearrange("p c t -> p (c t)"), H, "w1", "scale_win%d" % X)
 
         gain_sq = sbuf([P, PACK], F32, "gain_sq")
         gain_eps = sbuf([P, PACK], F32, "gain_eps")
@@ -135,13 +134,11 @@ def tile_picked_ypainn_sigmoid_p_kernel(
         nc.scalar.activation(gain_sign[:], gain_t[:], ACT.Sign)
 
         def squares_of(c, picked, banks):
-            squares = []
+            squares = sbuf([P, TILES, PACK, P], F32, "squares%d" % c)
             for j in range(TILES):
                 v = bank(banks[j], [P, H], "v%d%d" % (c, j))
                 product(v[:], picked, tiles[j], w1_mx, slice(0, H))
-                sq = sbuf([P, PACK, P], F32, "sq%d%d" % (c, j))
-                nc.scalar.activation(sq[:], v[:].rearrange("p (m t) -> p t m", t=PACK), ACT.Square)
-                squares.append(sq)
+                nc.scalar.activation(squares[:, j], v[:].rearrange("p (m t) -> p t m", t=PACK), ACT.Square)
             return squares
 
         x_mx = (gather_words(X, (0, HALF, S)), x_scale)
@@ -156,21 +153,23 @@ def tile_picked_ypainn_sigmoid_p_kernel(
         sum_banks = ((6, 7), (2, 1))
         lengths = [sbuf([P, PACK, HALF], BF16, "lengths%d" % h) for h in range(2)]
 
-        squares = (x_squares, y_squares, z_squares)
+        xy_squares = sbuf([P, PACK, P], F32, "xy_squares")
+        nc.vector.tensor_tensor(xy_squares[:], x_squares[:, 3], y_squares[:, 3], ALU.add)
 
         def sums_of(h, terms):
             sums = [bank(sum_banks[h][u], [P, 2, HALF], "sum%d%d" % (h, u)) for u in range(2)]
-            for c, jj in terms:
+            for i, (squares, jj) in enumerate(terms):
                 for t in range(PACK):
-                    nc.tensor.matmul(out=sums[t // 2][:, t % 2, tiles[jj]], lhsT=squares[c][2 * h + jj][:, t, :],
+                    nc.tensor.matmul(out=sums[t // 2][:, t % 2, tiles[jj]], lhsT=squares[:, t, :],
                                      rhs=ident[:], is_transpose=True,
-                                     start=((c, jj) == terms[0] and t % 2 == 0), stop=((c, jj) == terms[-1] and t % 2 == 1))
+                                     start=(i == 0 and t % 2 == 0), stop=(i == len(terms) - 1 and t % 2 == 1))
             for t in range(PACK):
                 nc.scalar.activation(lengths[h][:, t, :], sums[t // 2][:, t % 2, :], ACT.Sqrt,
                                      scale=gain_sq[:, t : t + 1], bias=gain_eps[:, t : t + 1])
 
-        sums_of(0, [(Y, 0), (X, 0), (X, 1), (Y, 1), (Z, 0), (Z, 1)])
-        sums_of(1, [(c, jj) for c in (X, Y, Z) for jj in range(2)])
+        sums_of(0, [(y_squares[:, 0], 0), (x_squares[:, 0], 0), (x_squares[:, 1], 1), (y_squares[:, 1], 1),
+                    (z_squares[:, 0], 0), (z_squares[:, 1], 1)])
+        sums_of(1, [(x_squares[:, 2], 0), (y_squares[:, 2], 0), (xy_squares[:], 1), (z_squares[:, 2], 0), (z_squares[:, 3], 1)])
         e_scale = gather_scales(E, "word_win%d" % Z)
 
         w23_bf = sbuf([P, 2, N, PACK], BF16, "w23_bf")

import math
from contextlib import ExitStack

import concourse.mybir as mybir
from concourse.masks import make_identity

F32 = mybir.dt.float32
BF16 = mybir.dt.bfloat16
I32 = mybir.dt.int32
U32 = mybir.dt.uint32
U16 = mybir.dt.uint16
U8 = mybir.dt.uint8
FP8X4 = mybir.dt.float8_e4m3fn_x4
ACT = mybir.ActivationFunctionType
ALU = mybir.AluOpType

P = 128
PACK = 4
K, T, S, H, N = 512, 2048, 512, 512, 128
HALF = S // 2
TILES = S // P
EPS = 0.05
W1_SCALAR_SHARE = 320
FLOPS = 2 * K * S * (3 * H + 7 * N) + 2 * H * S * N
X, Y, Z, E = range(4)


def tile_picked_ypainn_sigmoid_p_kernel(
    tc, x_words, x_scales, g_words, g_scales, d_words, d_scales, e_words, e_scales,
    w1, w2, w3, w4, w5, gain, skip, offs, out,
):
    nc = tc.nc
    words_in = (x_words, g_words, d_words, e_words)
    scales_in = (x_scales, g_scales, d_scales, e_scales)
    halves = [slice(h * HALF, (h + 1) * HALF) for h in range(2)]
    tiles = [slice(j * P, (j + 1) * P) for j in range(TILES)]

    with ExitStack() as ctx:
        keep = ctx.enter_context(tc.tile_pool(name="keep", bufs=1))
        psum = ctx.enter_context(tc.psum_pool(name="psum", bufs=1))

        def sbuf(shape, dtype, name, tag=None):
            return keep.tile(shape, dtype, name=name, tag=tag or name, align_bytes=64)

        def bank(b, shape, name):
            return psum.tile(shape, F32, name=name, tag="bank%d" % b)

        offsets = keep.tile([P, S // 16], U16, name="offsets")

        scale_win = [sbuf([P, T], U8, "scale_win%d" % c) for c in range(4)]
        nc.gpsimd.memset(scale_win[X][:].bitcast(I32), 0)
        for c in (Z, Y, E):
            nc.vector.memset(scale_win[c][:].bitcast(I32), 0)
        word_win = [sbuf([P, T], I32, "word_win%d" % c) for c in range(4)]

        one = sbuf([P, 1], F32, "one")
        nc.gpsimd.memset(one[:], 1.0)
        warm = sbuf([P, 1], F32, "warm")
        nc.scalar.activation(warm[:], one[:], ACT.Sqrt)
        ident = sbuf([P, P], F32, "ident")
        make_identity(nc, ident[:])

        def load_scales(c, queue):
            for r in range(4):
                queue.dma_start(scale_win[c][4 * c + r : P : 32, :].bitcast(I32),
                                scales_in[c][0, r:16:4, :].bitcast(I32))

        def load_words(c):
            nc.sync.dma_start(word_win[c][:], words_in[c][0].rearrange("p n t -> p (n t)").bitcast(I32))

        def by_slot(w):
            return w.rearrange("(p j) c -> p j c", j=PACK)

        w1_raw = sbuf([P, PACK, H], F32, "w1_raw")
        w23_raw = sbuf([P, 2, PACK, N], F32, "w23_raw")
        w4_raw = sbuf([P, PACK, N], F32, "w4_raw")
        w5_raw = sbuf([P, PACK, N], F32, "w5_raw")
        gain_t = sbuf([P, PACK], F32, "gain_t")
        skip_t = sbuf([P, S], F32, "skip_t")

        nc.sync.dma_start(w1_raw[:], by_slot(w1))
        nc.sync.dma_start(offsets[:], offs)
        load_scales(X, nc.sync)
        load_words(X)
        nc.sync.dma_start(gain_t[:], gain.rearrange("(p j) o -> p (j o)", j=PACK))
        load_scales(Y, nc.sync)
        load_words(Y)
        load_words(Z)
        nc.sync.dma_start(w23_raw[:, 0], by_slot(w2))
        nc.sync.dma_start(w23_raw[:, 1], by_slot(w3))
        nc.sync.dma_start(w4_raw[:], by_slot(w4))
        nc.sync.dma_start(w5_raw[:], by_slot(w5))
        load_words(E)
        nc.sync.dma_start(skip_t[:], skip)
        load_scales(Z, nc.gpsimd)
        load_scales(E, nc.gpsimd)

        def interleave(copy, grouped, planes):
            copy(grouped.rearrange("p (c i) t -> p c t i", i=4), planes.rearrange("p t (c i) -> p c t i", i=4))

        def quantize(values, width, name, tag=None):
            codes = sbuf([P, width], U32, name + "_codes", tag)
            scale = sbuf([P, width], U8, name + "_scale")
            nc.vector.quantize_mx(out=codes[:].bitcast(FP8X4), scales=scale[:], in_=values)
            return codes, scale

        def gather_scales(c, tag=None):
            scale = sbuf([P, S], U8, "picked_scale%d" % c, tag)
            nc.vector.tensor_copy(scale[:], scale_win[c][:].indirect(offsets[:]))
            return scale[4 * c : P]

        def gather_words(c, cuts):
            words = sbuf([P, S], U32, "picked_words%d" % c)
            for lo, hi in zip(cuts, cuts[1:]):
                nc.vector.tensor_copy(words[:, lo:hi], word_win[c][:].bitcast(U32).indirect(offsets[:, lo // 16 : hi // 16]))
            return words

        def product(result, lhs, lhs_cols, rhs, rhs_cols, start=True, stop=True):
            nc.tensor.matmul_mx(out=result, lhsT=lhs[0][:, lhs_cols].bitcast(FP8X4), lhsT_scale=lhs[1][:, lhs_cols],
                                rhs=rhs[0][:, rhs_cols].bitcast(FP8X4), rhs_scale=rhs[1][:, rhs_cols],
                                start=start, stop=stop)

        x_scale = gather_scales(X)
        w1_bf = sbuf([P, H, PACK], BF16, "w1_bf")
        interleave(nc.scalar.copy, w1_bf[:, :W1_SCALAR_SHARE, :], w1_raw[:, :, :W1_SCALAR_SHARE])
        interleave(nc.vector.tensor_copy, w1_bf[:, W1_SCALAR_SHARE:, :], w1_raw[:, :, W1_SCALAR_SHARE:])
        w1_mx = quantize(w1_bf[:].rearrange("p c t -> p (c t)"), H, "w1", "scale_win%d" % X)

        gain_sq = sbuf([P, PACK], F32, "gain_sq")
        gain_eps = sbuf([P, PACK], F32, "gain_eps")
        gain_sign = sbuf([P, PACK], F32, "gain_sign")
        nc.scalar.activation(gain_sq[:], gain_t[:], ACT.Square)
        nc.scalar.activation(gain_eps[:], gain_t[:], ACT.Square, scale=math.sqrt(EPS))
        nc.scalar.activation(gain_sign[:], gain_t[:], ACT.Sign)

        def squares_of(c, picked, banks):
            squares = sbuf([P, TILES, PACK, P], F32, "squares%d" % c)
            for j in range(TILES):
                v = bank(banks[j], [P, H], "v%d%d" % (c, j))
                product(v[:], picked, tiles[j], w1_mx, slice(0, H))
                nc.scalar.activation(squares[:, j], v[:].rearrange("p (m t) -> p t m", t=PACK), ACT.Square)
            return squares

        x_mx = (gather_words(X, (0, HALF, S)), x_scale)
        x_squares = squares_of(X, x_mx, (0, 1, 2, 3))
        y_scale = gather_scales(Y)
        y_mx = (gather_words(Y, (0, P, HALF, S)), y_scale)
        y_squares = squares_of(Y, y_mx, (4, 5, 0, 1))
        z_scale = gather_scales(Z, "word_win%d" % Y)
        z_mx = (gather_words(Z, (0, P, HALF, S)), z_scale)
        z_squares = squares_of(Z, z_mx, (2, 3, 4, 5))

        sum_banks = ((6, 7), (2, 1))
        lengths = [sbuf([P, PACK, HALF], BF16, "lengths%d" % h) for h in range(2)]

        xy_squares = sbuf([P, PACK, P], F32, "xy_squares")
        nc.vector.tensor_tensor(xy_squares[:], x_squares[:, 3], y_squares[:, 3], ALU.add)

        def sums_of(h, terms):
            sums = [bank(sum_banks[h][u], [P, 2, HALF], "sum%d%d" % (h, u)) for u in range(2)]
            for i, (squares, jj) in enumerate(terms):
                for t in range(PACK):
                    nc.tensor.matmul(out=sums[t // 2][:, t % 2, tiles[jj]], lhsT=squares[:, t, :],
                                     rhs=ident[:], is_transpose=True,
                                     start=(i == 0 and t % 2 == 0), stop=(i == len(terms) - 1 and t % 2 == 1))
            for t in range(PACK):
                nc.scalar.activation(lengths[h][:, t, :], sums[t // 2][:, t % 2, :], ACT.Sqrt,
                                     scale=gain_sq[:, t : t + 1], bias=gain_eps[:, t : t + 1])

        sums_of(0, [(y_squares[:, 0], 0), (x_squares[:, 0], 0), (x_squares[:, 1], 1), (y_squares[:, 1], 1),
                    (z_squares[:, 0], 0), (z_squares[:, 1], 1)])
        sums_of(1, [(x_squares[:, 2], 0), (y_squares[:, 2], 0), (xy_squares[:], 1), (z_squares[:, 2], 0), (z_squares[:, 3], 1)])
        e_scale = gather_scales(E, "word_win%d" % Z)

        w23_bf = sbuf([P, 2, N, PACK], BF16, "w23_bf")
        w4_bf = sbuf([P, N, PACK], BF16, "w4_bf")
        w5_bf = sbuf([P, N, PACK], BF16, "w5_bf")
        for i in range(2):
            nc.gpsimd.tensor_scalar(w23_bf[:, i], w23_raw[:, i].rearrange("p t c -> p c t"), 1.0, 0.0, ALU.mult, ALU.add)
        nc.vector.tensor_tensor(w4_bf[:].rearrange("p (c i) t -> p c t i", i=4),
                                w4_raw[:].rearrange("p t (c i) -> p c t i", i=4),
                                gain_sign[:].unsqueeze(1).unsqueeze(3).to_broadcast([P, N // 4, PACK, 4]), ALU.mult)
        w23_mx = quantize(w23_bf[:].rearrange("p a c t -> p (a c t)"), 2 * N, "w23")
        interleave(nc.vector.tensor_copy, w5_bf[:], w5_raw[:])
        w4_mx = quantize(w4_bf[:].rearrange("p c t -> p (c t)"), N, "w4")
        w5_mx = quantize(w5_bf[:].rearrange("p c t -> p (c t)"), N, "w5")

        ab_banks = ((0, 3, 4), (5, 6, 7))
        products = [sbuf([P, 3, 2, N], F32, "products%d" % h) for h in range(2)]

        def ab_of(h, c):
            ab = bank(ab_banks[h][c], [P, 2, 2 * N], "ab%d%d" % (c, h))
            for jj in range(2):
                product(ab[:, jj, :], (x_mx, y_mx, z_mx)[c], tiles[2 * h + jj], w23_mx, slice(0, 2 * N))
            return ab, sbuf([P, 2, N], F32, "b_half%d%d" % (c, h))

        def multiply(h, c, pair):
            nc.vector.tensor_tensor(products[h][:, c], pair[0][:, :, 0:N], pair[1][:], ALU.mult)

        e_mx = (gather_words(E, (0, S)), e_scale)
        pairs = {}
        keys = [(h, c) for h in range(2) for c in (X, Y, Z)]
        for key in keys:
            pairs[key] = ab_of(*key)
            nc.scalar.activation(pairs[key][1][:], pairs[key][0][:, :, N : 2 * N], ACT.Copy, scale=0.5)
        nrm = sbuf([P, S, PACK], BF16, "nrm")
        for h in range(2):
            interleave(nc.vector.tensor_copy, nrm[:, halves[h], :], lengths[h][:])
        multiply(*keys[0], pairs[keys[0]])
        nrm_mx = quantize(nrm[:].rearrange("p n t -> p (n t)"), S, "nrm")
        for key in keys[1:]:
            multiply(*key, pairs[key])

        gate = bank(2, [P, S], "gate")
        product(gate[:], w5_mx, slice(0, N), e_mx, slice(0, S), start=True, stop=False)
        product(gate[:], w4_mx, slice(0, N), nrm_mx, slice(0, S), start=False, stop=True)

        dots = [bank(3 * h, [P, HALF], "dot%d" % h) for h in range(2)]
        for h in range(2):
            for c in range(3):
                for jj in range(2):
                    nc.tensor.matmul(out=dots[h][:, tiles[jj]], lhsT=products[h][:, c, jj, :], rhs=ident[:],
                                     is_transpose=True, start=(c == 0 and jj == 0), stop=(c == 2 and jj == 1))

        sig = sbuf([P, S], F32, "sig")
        gated = sbuf([P, S], F32, "gated")
        res = sbuf([P, S], F32, "res")
        pieces = ((0, slice(0, HALF)), (1, tiles[0]), (1, tiles[1]))
        out_cols = (halves[0], tiles[2], tiles[3])
        for cols in out_cols:
            nc.scalar.activation(sig[:, cols], gate[:, cols], ACT.Sigmoid)

        def gate_piece(i):
            h, part = pieces[i]
            nc.vector.tensor_tensor(gated[:, out_cols[i]], dots[h][:, part], sig[:, out_cols[i]], ALU.mult)

        def store_piece(i):
            cols = out_cols[i]
            nc.vector.tensor_tensor(res[:, cols], gated[:, cols], skip_t[:, cols], ALU.add)
            nc.sync.dma_start(out[:, cols], res[:, cols])

        gate_piece(0)
        gate_piece(1)
        store_piece(0)
        gate_piece(2)
        store_piece(1)
        store_piece(2)
